import numpy as np
import ml_dtypes


def mxq(x, axis, fmt="e4m3"):
    dtype, down = {"e4m3": (ml_dtypes.float8_e4m3fn, 7), "e5m2": (ml_dtypes.float8_e5m2, 14)}[fmt]
    v = np.moveaxis(np.asarray(x, np.float32).astype(ml_dtypes.bfloat16).astype(np.float64), axis, -1)
    blocks = v.reshape(v.shape[:-1] + (-1, 32))
    amax = np.abs(blocks).max(-1, keepdims=True)
    byte = np.maximum(np.where(amax > 0, np.frexp(amax)[1] - 1 + 127, 0) - down, 1)
    scale = np.exp2(byte - 127.0)
    codes = (blocks / scale).astype(np.float32).astype(dtype).astype(np.float64)
    return np.moveaxis((codes * scale).reshape(v.shape), -1, axis)


WIDE = False


def mx_kscale(k):
    if not WIDE:
        return np.ones(k)
    levels = np.array([10, -10, 5, -5, 0])
    if k % 512:
        return np.exp2(np.random.permutation(np.resize(levels, k // 32))).repeat(32)
    a = np.empty((k // 512, 16))
    for p in range(k // 512):
        a[p, :8] = np.random.permutation(np.resize(levels, 8))
        for g in range(8):
            far = levels[np.abs(levels - a[p, g]) >= 10]
            a[p, g + 8] = far[np.random.randint(len(far))]
    return np.exp2(a.ravel()).repeat(32)


def f64(x):
    return np.asarray(x).astype(np.float64)


def striped(idx):
    return np.tile(idx.reshape(-1, 16).T, (8, 1)).astype(np.uint16)


def unstriped(offs):
    return offs[:16].T.reshape(-1).astype(np.int64)


E2M1 = np.array([0.0, 0.5, 1.0, 1.5, 2.0, 3.0, 4.0, 6.0, -0.0, -0.5, -1.0, -1.5, -2.0, -3.0, -4.0, -6.0])


def pack_weight(w, fmt):
    k, n = w.shape
    w = f64(np.asarray(w, np.float32).astype(ml_dtypes.bfloat16)).reshape(k // 32, 32, n)
    amax = np.abs(w).max(1)
    if fmt == "e4m3":
        byte = np.frexp(amax)[1] - 1 + 127 - 7
    else:
        mant, ex = np.frexp(amax / 6.0)
        byte = np.where(mant > 0.5, ex, ex - 1) + 127
    byte = np.clip(np.where(amax > 0, byte, 1), 1, 254)
    scaled = (w * np.exp2(127.0 - byte)[:, None, :]).reshape(k, n).astype(np.float32)
    by_word = np.ascontiguousarray(scaled.reshape(k // 512, 128, 4, n).transpose(0, 1, 3, 2))
    if fmt == "e4m3":
        words = by_word.astype(ml_dtypes.float8_e4m3fn).view(np.uint8)
    else:
        c = by_word.astype(ml_dtypes.float4_e2m1fn).view(np.uint8) & 0xF
        words = (c[..., 0::2] | (c[..., 1::2] << 4)).reshape(k // 512, 128, 2 * n)
    return np.ascontiguousarray(words), np.ascontiguousarray(byte.astype(np.uint8).reshape(k // 512, 16, n))


def unpack_weight(words, scales, fmt):
    g, _, n = scales.shape
    words = np.ascontiguousarray(words).reshape(g, 128, n, -1)
    if fmt == "e4m3":
        vals = words.view(ml_dtypes.float8_e4m3fn).astype(np.float64)
    else:
        nib = np.empty((g, 128, n, 4), np.uint8)
        nib[..., 0::2] = words & 0xF
        nib[..., 1::2] = words >> 4
        vals = E2M1[nib]
    vals = vals * np.repeat(np.exp2(scales.astype(np.float64) - 127.0), 8, axis=1)[..., None]
    return vals.transpose(0, 1, 3, 2).reshape(g * 512, n)


def gelu(v):
    return 0.5 * v * (1.0 + np.tanh(np.sqrt(2.0 / np.pi) * (v + 0.044715 * v**3)))


K, K2, H, N, T, T2, S = 1024, 512, 1024, 512, 2048, 2048, 1024

def setup_inputs():
    n = np.random.standard_normal
    s = mx_kscale(K)[:, None]
    s2 = mx_kscale(K2)[:, None]
    u = mx_kscale(H)[:, None]
    wa = (n((K, H)) / np.sqrt(K) / s * u.T).astype(np.float32)
    tab_words, tab_scales = pack_weight(n((K, T)) * s, "e4m3")
    tab2_words, tab2_scales = pack_weight(n((K2, T2)) * s2, "e4m3")
    wb_words, wb_scales = pack_weight(n((K2, H)) / np.sqrt(K2) / s2, "e2m1")
    wf_words, wf_scales = pack_weight(n((H, N)) / np.sqrt(H) / u, "e4m3")
    return {"wa": wa, "tab_words": tab_words, "tab_scales": tab_scales,
            "tab2_words": tab2_words, "tab2_scales": tab2_scales,
            "wb_words": wb_words, "wb_scales": wb_scales,
            "wf_words": wf_words, "wf_scales": wf_scales,
            "gT": (0.5 * n((H, T)) * u).astype(np.float32),
            "bias": (0.3 * n(N)).astype(np.float32),
            "offs": striped(np.random.permutation(T)[:S]),
            "offs2": striped(np.random.permutation(T2)[:S])}

def reference(wa, tab_words, tab_scales, tab2_words, tab2_scales, wb_words, wb_scales,
              wf_words, wf_scales, gT, bias, offs, offs2):
    v = unpack_weight(tab_words, tab_scales, "e4m3")[:, unstriped(offs)]
    v2 = unpack_weight(tab2_words, tab2_scales, "e4m3")[:, unstriped(offs2)]
    g = f64(gT)[:, unstriped(offs)]
    a = mxq(f64(wa), 0, "e4m3").T @ v
    wb = unpack_weight(wb_words, wb_scales, "e2m1")
    b = wb.T @ v2
    h = a / (1.0 + np.abs(b)) + g
    wf = unpack_weight(wf_words, wf_scales, "e4m3")
    y = wf.T @ mxq(h, 0, "e4m3")
    return y + f64(bias)[:, None]

@@ -1,0 +1,237 @@
+from contextlib import ExitStack
+
+import concourse.mybir as mybir
+
+K, K2, H, N, T, S = 1024, 512, 1024, 512, 2048, 1024
+FLOPS = 2 * S * (K * H + K2 * H + H * N)
+
+F32 = mybir.dt.float32
+BF16 = mybir.dt.bfloat16
+I32 = mybir.dt.int32
+U32 = mybir.dt.uint32
+U16 = mybir.dt.uint16
+U8 = mybir.dt.uint8
+FP8X4 = mybir.dt.float8_e4m3fn_x4
+FP4X4 = mybir.dt.float4_e2m1fn_x4
+ACT = mybir.ActivationFunctionType
+ALU = mybir.AluOpType
+
+P = 128
+W = 512
+ADD_ON_POOL = False
+CAST_ON_POOL = False
+
+
+def tile_list_regime_damped_signals_kernel(
+    tc, wa, tab_words, tab_scales, tab2_words, tab2_scales, wb_words, wb_scales,
+    wf_words, wf_scales, gT, bias, offs, offs2, out
+):
+    nc = tc.nc
+    with ExitStack() as ctx:
+        keep = ctx.enter_context(tc.tile_pool(name="keep", bufs=1))
+        big = ctx.enter_context(tc.tile_pool(name="big", bufs=10))
+        work = ctx.enter_context(tc.tile_pool(name="work", bufs=2))
+        psum = ctx.enter_context(tc.psum_pool(name="psum", bufs=2))
+
+        idx = keep.tile([P, S // 16], U16, name="idx")
+        idx2 = keep.tile([P, S // 16], U16, name="idx2")
+        v_sc_win = keep.tile([P, T // 4], I32, name="v_sc_win", align_bytes=64)
+        v2_sc_win = keep.tile([P, T // 4], I32, name="v2_sc_win", align_bytes=64)
+        wb_sc_raw = keep.tile([P, H // 4], I32, name="wb_sc_raw", align_bytes=64)
+        wf_sc = keep.tile([P, N // 4], I32, name="wf_sc", align_bytes=64)
+        wb_raw = keep.tile([P, H // 2], I32, name="wb_raw", align_bytes=64)
+        wb_codes = keep.tile([P, 2 * H], U8, name="wb_codes", align_bytes=64)
+        wb_sc = keep.tile([P, H], U8, name="wb_sc", align_bytes=64)
+        wf_codes = keep.tile([P, 2, N], I32, name="wf_codes", align_bytes=64)
+        bias_t = keep.tile([P, 4], F32, name="bias_t")
+        one = keep.tile([P, 1], F32, name="one")
+        warm = keep.tile([P, 1], F32, name="warm")
+        v_codes = keep.tile([P, 2, S], U32, name="v_codes", align_bytes=64)
+        v_sc = keep.tile([P, S], U8, name="v_sc", align_bytes=64)
+        v2_codes = keep.tile([P, S], U32, name="v2_codes", align_bytes=64)
+        v2_sc = keep.tile([P, S], U8, name="v2_sc", align_bytes=64)
+        wa_codes = keep.tile([P, 4, W], U32, name="wa_codes", align_bytes=64)
+        wa_sc = keep.tile([P, 4, W], U8, name="wa_sc", align_bytes=64)
+        h_codes = keep.tile([P, 4, W], U32, name="h_codes", align_bytes=64)
+        h_sc = keep.tile([P, 4, W], U8, name="h_sc", align_bytes=64)
+        damp = [keep.tile([P, 4, W], F32, name="damp%d" % u) for u in range(4)]
+        carry = [keep.tile([P, 4, W], F32, name="carry%d" % u) for u in range(4)]
+
+        nc.vector.memset(v2_sc_win[:], 0)
+        nc.vector.memset(wb_sc_raw[:], 0)
+        nc.vector.memset(v_sc_win[:], 0)
+        nc.gpsimd.memset(one[:], 1.0)
+        nc.gpsimd.memset(wf_sc[:], 0)
+        nc.scalar.activation(warm[:], one[:], ACT.Abs_reciprocal_sqrt, bias=one[:])
+
+        def big_tile(dtype, name):
+            return big.tile([P, T], dtype, name=name, tag="big", align_bytes=64)
+
+        nc.sync.dma_start(idx2[:], offs2)
+        for q in range(4):
+            nc.sync.dma_start(v2_sc_win[32 * q:32 * q + 4, :], tab2_scales[0, 4 * q:4 * q + 4, :].bitcast(I32))
+        nc.sync.dma_start(wb_raw[:], wb_words[0].bitcast(I32))
+        v2_win = big_tile(I32, "v2_win")
+        nc.sync.dma_start(v2_win[:], tab2_words[0].rearrange("p t i -> p (t i)").bitcast(I32))
+        nc.sync.dma_start(idx[:], offs)
+        for q in range(4):
+            nc.scalar.dma_start(wb_sc_raw[32 * q:32 * q + 4, :], wb_scales[0, 4 * q:4 * q + 4, :].bitcast(I32))
+        for q in range(4):
+            nc.sync.dma_start(v_sc_win[32 * q:32 * q + 8, :], tab_scales[:, 4 * q:4 * q + 4, :].bitcast(I32))
+        v_win = []
+        for a in range(2):
+            v_win.append(big_tile(I32, "v_win%d" % a))
+            nc.sync.dma_start(v_win[a][:], tab_words[a].rearrange("p t i -> p (t i)").bitcast(I32))
+        wa_raw = {}
+        g_win = {}
+        gT_v = gT.rearrange("(A p i) t -> A i p t", A=2, i=4)
+        wa_v = wa.rearrange("(a p j) r -> a p j r", a=2, j=4)
+        for A in range(2):
+            for a in range(2):
+                wa_raw[A, a] = big_tile(F32, "wa_raw%d%d" % (A, a))
+                nc.sync.dma_start(wa_raw[A, a][:].rearrange("p (j c) -> p j c", j=4), wa_v[a, :, :, A * W:(A + 1) * W])
+            for t in range(4):
+                g_win[A, t] = big_tile(F32, "g_win%d%d" % (A, t))
+                nc.sync.dma_start(g_win[A, t][:], gT_v[A, t])
+            if A == 0:
+                for q in range(4):
+                    nc.sync.dma_start(wf_sc[32 * q:32 * q + 8, :], wf_scales[:, 4 * q:4 * q + 4, :].bitcast(I32))
+                nc.sync.dma_start(wf_codes[:], wf_words.rearrange("a p e i -> p a (e i)").bitcast(I32))
+                with nc.allow_non_contiguous_dma(reason="one bias value a partition"):
+                    nc.sync.dma_start(bias_t[:], bias.rearrange("(c p) -> p c", p=P))
+
+        def cols(half):
+            return slice(half * W, (half + 1) * W)
+
+        def part(lst, half):
+            return lst[:, half * (W // 16):(half + 1) * (W // 16)]
+
+        nc.vector.tensor_copy(v2_sc[:, cols(0)], v2_sc_win[:].bitcast(U8).indirect(part(idx2, 0)))
+        nc.vector.tensor_copy(
+            wb_codes[:].bitcast(U16).rearrange("p (A t m) -> p A t m", A=2, t=4),
+            wb_raw[:].bitcast(U16).rearrange("p (A m t) -> p A t m", A=2, t=4))
+        nc.vector.tensor_copy(
+            wb_sc[:].rearrange("p (A t m) -> p A t m", A=2, t=4),
+            wb_sc_raw[:].bitcast(U8).rearrange("p (A m t) -> p A t m", A=2, t=4))
+        nc.vector.tensor_copy(v2_codes[:, cols(0)], v2_win[:].bitcast(U32).indirect(part(idx2, 0)))
+        nc.vector.tensor_copy(v2_sc[:, cols(1)], v2_sc_win[:].bitcast(U8).indirect(part(idx2, 1)))
+        nc.vector.tensor_copy(v2_codes[:, cols(1)], v2_win[:].bitcast(U32).indirect(part(idx2, 1)))
+
+        def damping(A, half):
+            d = damp[2 * A + half]
+            for t in range(4):
+                u = 4 * A + t
+                b_ps = psum.tile([P, W], F32, name="b_ps")
+                nc.tensor.matmul_mx(
+                    b_ps[:], lhsT=wb_codes[:, 256 * u:256 * (u + 1)].bitcast(FP4X4), lhsT_scale=wb_sc[:, P * u:P * (u + 1)],
+                    rhs=v2_codes[:, cols(half)].bitcast(FP8X4), rhs_scale=v2_sc[:, cols(half)], start=True, stop=True)
+                nc.scalar.activation(d[:, t, :], b_ps[:], ACT.Abs)
+            for t in (0, 2):
+                nc.scalar.activation(d[:, t:t + 2, :], d[:, t:t + 2, :], ACT.Abs_reciprocal_sqrt, bias=one[:])
+            for t in (0, 2):
+                nc.scalar.activation(d[:, t:t + 2, :], d[:, t:t + 2, :], ACT.Square)
+
+        def cast_wa(A):
+            tiles = []
+            for a in range(2):
+                grouped = work.tile([P, 4 * W], BF16, name="wa_grouped", align_bytes=64)
+                dst = grouped[:].rearrange("p (t m j) -> p m t j", t=4, j=4)
+                src = wa_raw[A, a][:].rearrange("p (j m t) -> p m t j", j=4, t=4)
+                if CAST_ON_POOL:
+                    nc.gpsimd.tensor_scalar(dst, src, 1.0, 0.0, ALU.mult, ALU.add)
+                else:
+                    nc.scalar.copy(dst, src)
+                tiles.append(grouped)
+            return tiles
+
+        def quantise_wa(A, tiles):
+            for a in range(2):
+                nc.vector.quantize_mx(wa_codes[:, 2 * A + a, :].bitcast(FP8X4), wa_sc[:, 2 * A + a, :], tiles[a][:])
+
+        def gather_carry(A, half):
+            for t in range(4):
+                nc.vector.tensor_copy(carry[2 * A + half][:, t, :], g_win[A, t][:].indirect(part(idx, half)))
+
+        def loadings(A, half):
+            d = damp[2 * A + half]
+            for t in range(4):
+                a_ps = psum.tile([P, W], F32, name="a_ps")
+                for a in range(2):
+                    nc.tensor.matmul_mx(
+                        a_ps[:], lhsT=wa_codes[:, 2 * A + a, P * t:P * (t + 1)].bitcast(FP8X4),
+                        lhsT_scale=wa_sc[:, 2 * A + a, P * t:P * (t + 1)],
+                        rhs=v_codes[:, a, cols(half)].bitcast(FP8X4), rhs_scale=v_sc[4 * a:P, cols(half)],
+                        start=(a == 0), stop=(a == 1))
+                nc.vector.tensor_tensor(d[:, t, :], a_ps[:], d[:, t, :], ALU.mult)
+
+        def exposures(A, half):
+            u = 2 * A + half
+            hb = work.tile([P, 4 * W], BF16, name="h_bf16", align_bytes=64)
+            dst = hb[:].rearrange("p (c i t) -> p c t i", i=4, t=4)
+            q = damp[u][:].rearrange("p t (c i) -> p c t i", i=4)
+            g = carry[u][:].rearrange("p t (c i) -> p c t i", i=4)
+            if ADD_ON_POOL:
+                for c0 in range(0, 128, 32):
+                    nc.gpsimd.tensor_tensor(dst[:, c0:c0 + 32], q[:, c0:c0 + 32], g[:, c0:c0 + 32], ALU.add)
+            else:
+                nc.vector.tensor_tensor(dst, q, g, ALU.add)
+            return hb
+
+        def quantise_h(A, half, hb):
+            u = 2 * A + half
+            nc.vector.quantize_mx(h_codes[:, u, :].bitcast(FP8X4), h_sc[:, u, :], hb[:])
+
+        y_ps = {}
+
+        def signals(A, half):
+            for c in range(4):
+                if A == 0:
+                    y_ps[c] = psum.tile([P, W], F32, name="y_ps", bufs=4)
+                nc.tensor.matmul_mx(
+                    y_ps[c][:], lhsT=wf_codes[:, A, P * c:P * (c + 1)].bitcast(FP8X4),
+                    lhsT_scale=wf_sc[:].bitcast(U8)[4 * A:P, P * c:P * (c + 1)],
+                    rhs=h_codes[:, 2 * A + half, :].bitcast(FP8X4), rhs_scale=h_sc[:, 2 * A + half, :],
+                    start=(A == 0), stop=(A == 1))
+
+        def store(half):
+            for c in range(4):
+                y = work.tile([P, W], F32, name="y", bufs=4)
+                if half == 1 and c % 2 == 1:
+                    nc.vector.tensor_scalar(y[:], y_ps[c][:], bias_t[:, c:c + 1], None, ALU.add)
+                else:
+                    nc.scalar.activation(y[:], y_ps[c][:], ACT.Identity, bias=bias_t[:, c:c + 1])
+                nc.sync.dma_start(out[P * c:P * (c + 1), cols(half)], y[:])
+
+        damping(0, 0)
+        nc.vector.tensor_copy(v_sc[:], v_sc_win[:].bitcast(U8).indirect(idx[:]))
+        for a in range(2):
+            nc.vector.tensor_copy(v_codes[:, a, :], v_win[a][:].bitcast(U32).indirect(idx[:]))
+        grouped0 = cast_wa(0)
+        damping(0, 1)
+        quantise_wa(0, grouped0)
+        gather_carry(0, 0)
+        loadings(0, 0)
+        h00 = exposures(0, 0)
+        grouped1 = cast_wa(1)
+        damping(1, 0)
+        gather_carry(0, 1)
+        quantise_h(0, 0, h00)
+        loadings(0, 1)
+        h01 = exposures(0, 1)
+        quantise_wa(1, grouped1)
+        damping(1, 1)
+        signals(0, 0)
+        gather_carry(1, 0)
+        quantise_h(0, 1, h01)
+        loadings(1, 0)
+        h10 = exposures(1, 0)
+        gather_carry(1, 1)
+        quantise_h(1, 0, h10)
+        signals(1, 0)
+        store(0)
+        signals(0, 1)
+        loadings(1, 1)
+        h11 = exposures(1, 1)
+        quantise_h(1, 1, h11)
+        signals(1, 1)
+        store(1)

@@ -19,7 +19,7 @@ ALU = mybir.AluOpType
 P = 128
 W = 512
 ADD_ON_POOL = False
-CAST_ON_POOL = False
+CAST_ON_POOL = True
 
 
 def tile_list_regime_damped_signals_kernel(
@@ -31,7 +31,7 @@ def tile_list_regime_damped_signals_kernel(
         keep = ctx.enter_context(tc.tile_pool(name="keep", bufs=1))
         big = ctx.enter_context(tc.tile_pool(name="big", bufs=10))
         work = ctx.enter_context(tc.tile_pool(name="work", bufs=2))
-        psum = ctx.enter_context(tc.psum_pool(name="psum", bufs=2))
+        psum = ctx.enter_context(tc.psum_pool(name="psum", bufs=4))
 
         idx = keep.tile([P, S // 16], U16, name="idx")
         idx2 = keep.tile([P, S // 16], U16, name="idx2")
@@ -54,30 +54,34 @@ def tile_list_regime_damped_signals_kernel(
         wa_sc = keep.tile([P, 4, W], U8, name="wa_sc", align_bytes=64)
         h_codes = keep.tile([P, 4, W], U32, name="h_codes", align_bytes=64)
         h_sc = keep.tile([P, 4, W], U8, name="h_sc", align_bytes=64)
-        damp = [keep.tile([P, 4, W], F32, name="damp%d" % u) for u in range(4)]
-        carry = [keep.tile([P, 4, W], F32, name="carry%d" % u) for u in range(4)]
-
-        nc.vector.memset(v2_sc_win[:], 0)
-        nc.vector.memset(wb_sc_raw[:], 0)
-        nc.vector.memset(v_sc_win[:], 0)
-        nc.gpsimd.memset(one[:], 1.0)
-        nc.gpsimd.memset(wf_sc[:], 0)
-        nc.scalar.activation(warm[:], one[:], ACT.Abs_reciprocal_sqrt, bias=one[:])
+        damp = [keep.tile([P, 4, W], F32, name="damp%d" % u, tag="damp%d" % u) for u in range(4)]
+        carry01 = keep.tile([P, 4, S], F32, name="carry01")
+        carry2 = keep.tile([P, 4, W], F32, name="carry2")
+        carry = {0: carry01[:, :, 0:W], 1: carry01[:, :, W:S], 2: carry2[:]}
+        damped_t = [damp[0], damp[1], damp[2], keep.tile([P, 4, W], F32, name="damped3")]
 
         def big_tile(dtype, name):
             return big.tile([P, T], dtype, name=name, tag="big", align_bytes=64)
 
+        nc.vector.memset(v_sc_win[:], 0)
+        nc.gpsimd.memset(one[:], 1.0)
+        nc.gpsimd.memset(wf_sc[:], 0)
+
+        def load_plane(tile, rows):
+            for q in range(4):
+                four = rows[4 * q:4 * q + 4, :].bitcast(I32)
+                nc.sync.dma_start(tile[32 * q:32 * q + 32, :], four.unsqueeze(0).broadcast_to([8, 4, four.shape[1]]))
+
         nc.sync.dma_start(idx2[:], offs2)
-        for q in range(4):
-            nc.sync.dma_start(v2_sc_win[32 * q:32 * q + 4, :], tab2_scales[0, 4 * q:4 * q + 4, :].bitcast(I32))
+        load_plane(v2_sc_win, tab2_scales[0])
         nc.sync.dma_start(wb_raw[:], wb_words[0].bitcast(I32))
         v2_win = big_tile(I32, "v2_win")
         nc.sync.dma_start(v2_win[:], tab2_words[0].rearrange("p t i -> p (t i)").bitcast(I32))
         nc.sync.dma_start(idx[:], offs)
-        for q in range(4):
-            nc.scalar.dma_start(wb_sc_raw[32 * q:32 * q + 4, :], wb_scales[0, 4 * q:4 * q + 4, :].bitcast(I32))
+        load_plane(wb_sc_raw, wb_scales[0])
         for q in range(4):
             nc.sync.dma_start(v_sc_win[32 * q:32 * q + 8, :], tab_scales[:, 4 * q:4 * q + 4, :].bitcast(I32))
+        nc.scalar.activation(warm[:], one[:], ACT.Abs_reciprocal_sqrt, bias=one[:])
         v_win = []
         for a in range(2):
             v_win.append(big_tile(I32, "v_win%d" % a))
@@ -86,19 +90,30 @@ def tile_list_regime_damped_signals_kernel(
         g_win = {}
         gT_v = gT.rearrange("(A p i) t -> A i p t", A=2, i=4)
         wa_v = wa.rearrange("(a p j) r -> a p j r", a=2, j=4)
-        for A in range(2):
-            for a in range(2):
-                wa_raw[A, a] = big_tile(F32, "wa_raw%d%d" % (A, a))
-                nc.sync.dma_start(wa_raw[A, a][:].rearrange("p (j c) -> p j c", j=4), wa_v[a, :, :, A * W:(A + 1) * W])
-            for t in range(4):
-                g_win[A, t] = big_tile(F32, "g_win%d%d" % (A, t))
-                nc.sync.dma_start(g_win[A, t][:], gT_v[A, t])
-            if A == 0:
-                for q in range(4):
-                    nc.sync.dma_start(wf_sc[32 * q:32 * q + 8, :], wf_scales[:, 4 * q:4 * q + 4, :].bitcast(I32))
-                nc.sync.dma_start(wf_codes[:], wf_words.rearrange("a p e i -> p a (e i)").bitcast(I32))
-                with nc.allow_non_contiguous_dma(reason="one bias value a partition"):
-                    nc.sync.dma_start(bias_t[:], bias.rearrange("(c p) -> p c", p=P))
+
+        def load_wa(A, a):
+            wa_raw[A, a] = big_tile(F32, "wa_raw%d%d" % (A, a))
+            nc.sync.dma_start(wa_raw[A, a][:].rearrange("p (j c) -> p j c", j=4), wa_v[a, :, :, A * W:(A + 1) * W])
+
+        def load_g(A, t):
+            g_win[A, t] = big_tile(F32, "g_win%d%d" % (A, t))
+            nc.sync.dma_start(g_win[A, t][:], gT_v[A, t])
+
+        load_wa(0, 0)
+        load_wa(0, 1)
+        load_g(0, 0)
+        load_g(0, 1)
+        load_wa(1, 0)
+        load_g(0, 2)
+        load_wa(1, 1)
+        load_g(0, 3)
+        for q in range(4):
+            nc.sync.dma_start(wf_sc[32 * q:32 * q + 8, :], wf_scales[:, 4 * q:4 * q + 4, :].bitcast(I32))
+        with nc.allow_non_contiguous_dma(reason="one bias value a partition"):
+            nc.sync.dma_start(bias_t[:], bias.rearrange("(c p) -> p c", p=P))
+        for t in range(4):
+            load_g(1, t)
+        nc.sync.dma_start(wf_codes[:], wf_words.rearrange("a p e i -> p a (e i)").bitcast(I32))
 
         def cols(half):
             return slice(half * W, (half + 1) * W)
@@ -106,22 +121,28 @@ def tile_list_regime_damped_signals_kernel(
         def part(lst, half):
             return lst[:, half * (W // 16):(half + 1) * (W // 16)]
 
-        nc.vector.tensor_copy(v2_sc[:, cols(0)], v2_sc_win[:].bitcast(U8).indirect(part(idx2, 0)))
-        nc.vector.tensor_copy(
-            wb_codes[:].bitcast(U16).rearrange("p (A t m) -> p A t m", A=2, t=4),
-            wb_raw[:].bitcast(U16).rearrange("p (A m t) -> p A t m", A=2, t=4))
-        nc.vector.tensor_copy(
-            wb_sc[:].rearrange("p (A t m) -> p A t m", A=2, t=4),
-            wb_sc_raw[:].bitcast(U8).rearrange("p (A m t) -> p A t m", A=2, t=4))
-        nc.vector.tensor_copy(v2_codes[:, cols(0)], v2_win[:].bitcast(U32).indirect(part(idx2, 0)))
-        nc.vector.tensor_copy(v2_sc[:, cols(1)], v2_sc_win[:].bitcast(U8).indirect(part(idx2, 1)))
-        nc.vector.tensor_copy(v2_codes[:, cols(1)], v2_win[:].bitcast(U32).indirect(part(idx2, 1)))
+        def permute_wb(A):
+            nc.vector.tensor_copy(
+                wb_codes[:].bitcast(U16)[:, cols(A)].rearrange("p (t m) -> p t m", t=4),
+                wb_raw[:].bitcast(U16)[:, cols(A)].rearrange("p (m t) -> p t m", t=4))
+            nc.vector.tensor_copy(
+                wb_sc[:, cols(A)].rearrange("p (t m) -> p t m", t=4),
+                wb_sc_raw[:].bitcast(U8)[:, cols(A)].rearrange("p (m t) -> p t m", t=4))
+
+        def gather_regimes(half):
+            nc.vector.tensor_copy(v2_codes[:, cols(half)], v2_win[:].bitcast(U32).indirect(part(idx2, half)))
+            nc.vector.tensor_copy(v2_sc[:, cols(half)], v2_sc_win[:].bitcast(U8).indirect(part(idx2, half)))
+
+        gather_regimes(0)
+        permute_wb(0)
+        gather_regimes(1)
+        permute_wb(1)
 
         def damping(A, half):
             d = damp[2 * A + half]
             for t in range(4):
                 u = 4 * A + t
-                b_ps = psum.tile([P, W], F32, name="b_ps")
+                b_ps = psum.tile([P, W], F32, name="b_ps", tag="x")
                 nc.tensor.matmul_mx(
                     b_ps[:], lhsT=wb_codes[:, 256 * u:256 * (u + 1)].bitcast(FP4X4), lhsT_scale=wb_sc[:, P * u:P * (u + 1)],
                     rhs=v2_codes[:, cols(half)].bitcast(FP8X4), rhs_scale=v2_sc[:, cols(half)], start=True, stop=True)
@@ -134,7 +155,7 @@ def tile_list_regime_damped_signals_kernel(
         def cast_wa(A):
             tiles = []
             for a in range(2):
-                grouped = work.tile([P, 4 * W], BF16, name="wa_grouped", align_bytes=64)
+                grouped = work.tile([P, 4 * W], BF16, name="wa_grouped", align_bytes=64, bufs=3)
                 dst = grouped[:].rearrange("p (t m j) -> p m t j", t=4, j=4)
                 src = wa_raw[A, a][:].rearrange("p (j m t) -> p m t j", j=4, t=4)
                 if CAST_ON_POOL:
@@ -148,90 +169,117 @@ def tile_list_regime_damped_signals_kernel(
             for a in range(2):
                 nc.vector.quantize_mx(wa_codes[:, 2 * A + a, :].bitcast(FP8X4), wa_sc[:, 2 * A + a, :], tiles[a][:])
 
-        def gather_carry(A, half):
-            for t in range(4):
-                nc.vector.tensor_copy(carry[2 * A + half][:, t, :], g_win[A, t][:].indirect(part(idx, half)))
+        def gather_carry(u, t, j0=0, j1=W):
+            base = (u % 2) * W
+            nc.vector.tensor_copy(carry[u][:, t, j0:j1], g_win[u // 2, t][:].indirect(idx[:, (base + j0) // 16:(base + j1) // 16]))
 
-        def loadings(A, half):
-            d = damp[2 * A + half]
+        def gather_carry01(t):
+            nc.vector.tensor_copy(carry01[:, t, :], g_win[0, t][:].indirect(idx[:]))
+
+        a_ps = {}
+
+        def loadings(u):
+            A, half = divmod(u, 2)
             for t in range(4):
-                a_ps = psum.tile([P, W], F32, name="a_ps")
+                a_ps[u, t] = psum.tile([P, W], F32, name="a_ps", tag=("x" if u == 3 else "z"))
                 for a in range(2):
                     nc.tensor.matmul_mx(
-                        a_ps[:], lhsT=wa_codes[:, 2 * A + a, P * t:P * (t + 1)].bitcast(FP8X4),
+                        a_ps[u, t][:], lhsT=wa_codes[:, 2 * A + a, P * t:P * (t + 1)].bitcast(FP8X4),
                         lhsT_scale=wa_sc[:, 2 * A + a, P * t:P * (t + 1)],
                         rhs=v_codes[:, a, cols(half)].bitcast(FP8X4), rhs_scale=v_sc[4 * a:P, cols(half)],
                         start=(a == 0), stop=(a == 1))
-                nc.vector.tensor_tensor(d[:, t, :], a_ps[:], d[:, t, :], ALU.mult)
 
-        def exposures(A, half):
-            u = 2 * A + half
-            hb = work.tile([P, 4 * W], BF16, name="h_bf16", align_bytes=64)
-            dst = hb[:].rearrange("p (c i t) -> p c t i", i=4, t=4)
-            q = damp[u][:].rearrange("p t (c i) -> p c t i", i=4)
-            g = carry[u][:].rearrange("p t (c i) -> p c t i", i=4)
-            if ADD_ON_POOL:
-                for c0 in range(0, 128, 32):
-                    nc.gpsimd.tensor_tensor(dst[:, c0:c0 + 32], q[:, c0:c0 + 32], g[:, c0:c0 + 32], ALU.add)
-            else:
-                nc.vector.tensor_tensor(dst, q, g, ALU.add)
-            return hb
+        def damped(u, t):
+            nc.vector.tensor_tensor(damped_t[u][:, t, :], a_ps[u, t][:], damp[u][:, t, :], ALU.mult)
 
-        def quantise_h(A, half, hb):
-            u = 2 * A + half
-            nc.vector.quantize_mx(h_codes[:, u, :].bitcast(FP8X4), h_sc[:, u, :], hb[:])
+        h_bf16 = {}
+
+        def exposures(u, eng, c0, c1):
+            if u not in h_bf16:
+                h_bf16[u] = work.tile([P, 4 * W], BF16, name="h_bf16", align_bytes=64)
+            dst = h_bf16[u][:].rearrange("p (c i t) -> p c t i", i=4, t=4)
+            q = damped_t[u][:].rearrange("p t (c i) -> p c t i", i=4)
+            g = carry[u].rearrange("p t (c i) -> p c t i", i=4)
+            eng.tensor_tensor(dst[:, c0:c1], q[:, c0:c1], g[:, c0:c1], ALU.add)
+
+        def quantise_h(u, j0, j1):
+            nc.vector.quantize_mx(h_codes[:, u, j0:j1].bitcast(FP8X4), h_sc[:, u, j0:j1], h_bf16[u][:, 4 * j0:4 * j1])
 
         y_ps = {}
 
-        def signals(A, half):
+        def signals(A, half, j0, j1, tag):
             for c in range(4):
                 if A == 0:
-                    y_ps[c] = psum.tile([P, W], F32, name="y_ps", bufs=4)
+                    y_ps[half, j0, c] = psum.tile([P, j1 - j0], F32, name="y_ps", tag=tag)
                 nc.tensor.matmul_mx(
-                    y_ps[c][:], lhsT=wf_codes[:, A, P * c:P * (c + 1)].bitcast(FP8X4),
+                    y_ps[half, j0, c][:], lhsT=wf_codes[:, A, P * c:P * (c + 1)].bitcast(FP8X4),
                     lhsT_scale=wf_sc[:].bitcast(U8)[4 * A:P, P * c:P * (c + 1)],
-                    rhs=h_codes[:, 2 * A + half, :].bitcast(FP8X4), rhs_scale=h_sc[:, 2 * A + half, :],
+                    rhs=h_codes[:, 2 * A + half, j0:j1].bitcast(FP8X4), rhs_scale=h_sc[:, 2 * A + half, j0:j1],
                     start=(A == 0), stop=(A == 1))
 
-        def store(half):
+        def store(half, j0, j1, share):
             for c in range(4):
-                y = work.tile([P, W], F32, name="y", bufs=4)
-                if half == 1 and c % 2 == 1:
-                    nc.vector.tensor_scalar(y[:], y_ps[c][:], bias_t[:, c:c + 1], None, ALU.add)
+                y = work.tile([P, j1 - j0], F32, name="y", bufs=4)
+                if share and c % 2 == 1:
+                    nc.vector.tensor_scalar(y[:], y_ps[half, j0, c][:], bias_t[:, c:c + 1], None, ALU.add)
                 else:
-                    nc.scalar.activation(y[:], y_ps[c][:], ACT.Identity, bias=bias_t[:, c:c + 1])
-                nc.sync.dma_start(out[P * c:P * (c + 1), cols(half)], y[:])
+                    nc.scalar.activation(y[:], y_ps[half, j0, c][:], ACT.Identity, bias=bias_t[:, c:c + 1])
+                nc.sync.dma_start(out[P * c:P * (c + 1), half * W + j0:half * W + j1], y[:])
 
+        V = nc.vector
+        G = nc.gpsimd
         damping(0, 0)
+        damping(0, 1)
+        damping(1, 0)
+        damping(1, 1)
         nc.vector.tensor_copy(v_sc[:], v_sc_win[:].bitcast(U8).indirect(idx[:]))
         for a in range(2):
             nc.vector.tensor_copy(v_codes[:, a, :], v_win[a][:].bitcast(U32).indirect(idx[:]))
         grouped0 = cast_wa(0)
-        damping(0, 1)
         quantise_wa(0, grouped0)
-        gather_carry(0, 0)
-        loadings(0, 0)
-        h00 = exposures(0, 0)
+        loadings(0)
         grouped1 = cast_wa(1)
-        damping(1, 0)
-        gather_carry(0, 1)
-        quantise_h(0, 0, h00)
-        loadings(0, 1)
-        h01 = exposures(0, 1)
+        for t in range(4):
+            gather_carry01(t)
+        for t in range(4):
+            damped(0, t)
+        loadings(1)
+        for c0 in range(0, 128, 32):
+            exposures(0, G, c0, c0 + 32)
+        for t in range(4):
+            damped(1, t)
         quantise_wa(1, grouped1)
-        damping(1, 1)
-        signals(0, 0)
-        gather_carry(1, 0)
-        quantise_h(0, 1, h01)
-        loadings(1, 0)
-        h10 = exposures(1, 0)
-        gather_carry(1, 1)
-        quantise_h(1, 0, h10)
-        signals(1, 0)
-        store(0)
-        signals(0, 1)
-        loadings(1, 1)
-        h11 = exposures(1, 1)
-        quantise_h(1, 1, h11)
-        signals(1, 1)
-        store(1)
+        loadings(2)
+        loadings(3)
+        for c0 in range(0, 128, 32):
+            exposures(1, G, c0, c0 + 32)
+        for t in range(4):
+            gather_carry(2, t)
+        quantise_h(0, 0, W)
+        for t in range(4):
+            damped(2, t)
+        signals(0, 0, 0, W, "z")
+        quantise_h(1, 0, W)
+        for c0 in range(0, 128, 32):
+            exposures(2, G, c0, c0 + 32)
+        for t in range(4):
+            damped(3, t)
+        signals(0, 1, 0, 256, "x")
+        carry3 = keep.tile([P, 4, W], F32, name="carry3", tag="damp3")
+        carry[3] = carry3[:]
+        for t in range(4):
+            gather_carry(3, t, 0, 256)
+        quantise_h(2, 0, W)
+        signals(1, 0, 0, W, "z")
+        store(0, 0, W, False)
+        exposures(3, V, 0, 64)
+        for t in range(4):
+            gather_carry(3, t, 256, W)
+        quantise_h(3, 0, 256)
+        signals(1, 1, 0, 256, "x")
+        signals(0, 1, 256, W, "z")
+        exposures(3, V, 64, 128)
+        store(1, 0, 256, False)
+        quantise_h(3, 256, W)
+        signals(1, 1, 256, W, "z")
+        store(1, 256, W, True)

@@ -18,8 +18,6 @@ ALU = mybir.AluOpType
 
 P = 128
 W = 512
-ADD_ON_POOL = False
-CAST_ON_POOL = True
 
 
 def tile_list_regime_damped_signals_kernel(
@@ -29,7 +27,7 @@ def tile_list_regime_damped_signals_kernel(
     nc = tc.nc
     with ExitStack() as ctx:
         keep = ctx.enter_context(tc.tile_pool(name="keep", bufs=1))
-        big = ctx.enter_context(tc.tile_pool(name="big", bufs=10))
+        slots = ctx.enter_context(tc.tile_pool(name="slots", bufs=1))
         work = ctx.enter_context(tc.tile_pool(name="work", bufs=2))
         psum = ctx.enter_context(tc.psum_pool(name="psum", bufs=4))
 
@@ -52,16 +50,10 @@ def tile_list_regime_damped_signals_kernel(
         v2_sc = keep.tile([P, S], U8, name="v2_sc", align_bytes=64)
         wa_codes = keep.tile([P, 4, W], U32, name="wa_codes", align_bytes=64)
         wa_sc = keep.tile([P, 4, W], U8, name="wa_sc", align_bytes=64)
-        h_codes = keep.tile([P, 4, W], U32, name="h_codes", align_bytes=64)
         h_sc = keep.tile([P, 4, W], U8, name="h_sc", align_bytes=64)
-        damp = [keep.tile([P, 4, W], F32, name="damp%d" % u, tag="damp%d" % u) for u in range(4)]
-        carry01 = keep.tile([P, 4, S], F32, name="carry01")
-        carry2 = keep.tile([P, 4, W], F32, name="carry2")
-        carry = {0: carry01[:, :, 0:W], 1: carry01[:, :, W:S], 2: carry2[:]}
-        damped_t = [damp[0], damp[1], damp[2], keep.tile([P, 4, W], F32, name="damped3")]
 
-        def big_tile(dtype, name):
-            return big.tile([P, T], dtype, name=name, tag="big", align_bytes=64)
+        def slot_tile(slot, shape, dtype, name):
+            return slots.tile(shape, dtype, name=name, tag="slot%d" % slot, align_bytes=64)
 
         nc.vector.memset(v_sc_win[:], 0)
         nc.gpsimd.memset(one[:], 1.0)
@@ -72,48 +64,41 @@ def tile_list_regime_damped_signals_kernel(
                 four = rows[4 * q:4 * q + 4, :].bitcast(I32)
                 nc.sync.dma_start(tile[32 * q:32 * q + 32, :], four.unsqueeze(0).broadcast_to([8, 4, four.shape[1]]))
 
-        nc.sync.dma_start(idx2[:], offs2)
-        load_plane(v2_sc_win, tab2_scales[0])
-        nc.sync.dma_start(wb_raw[:], wb_words[0].bitcast(I32))
-        v2_win = big_tile(I32, "v2_win")
-        nc.sync.dma_start(v2_win[:], tab2_words[0].rearrange("p t i -> p (t i)").bitcast(I32))
-        nc.sync.dma_start(idx[:], offs)
-        load_plane(wb_sc_raw, wb_scales[0])
-        for q in range(4):
-            nc.sync.dma_start(v_sc_win[32 * q:32 * q + 8, :], tab_scales[:, 4 * q:4 * q + 4, :].bitcast(I32))
-        nc.scalar.activation(warm[:], one[:], ACT.Abs_reciprocal_sqrt, bias=one[:])
-        v_win = []
-        for a in range(2):
-            v_win.append(big_tile(I32, "v_win%d" % a))
-            nc.sync.dma_start(v_win[a][:], tab_words[a].rearrange("p t i -> p (t i)").bitcast(I32))
+        def load_words(slot, words, name):
+            win = slot_tile(slot, [P, T], I32, name)
+            nc.sync.dma_start(win[:], words.rearrange("p t i -> p (t i)").bitcast(I32))
+            return win
+
         wa_raw = {}
         g_win = {}
         gT_v = gT.rearrange("(A p i) t -> A i p t", A=2, i=4)
         wa_v = wa.rearrange("(a p j) r -> a p j r", a=2, j=4)
 
-        def load_wa(A, a):
-            wa_raw[A, a] = big_tile(F32, "wa_raw%d%d" % (A, a))
-            nc.sync.dma_start(wa_raw[A, a][:].rearrange("p (j c) -> p j c", j=4), wa_v[a, :, :, A * W:(A + 1) * W])
+        def load_wa(slot, A, a):
+            wa_raw[A, a] = slot_tile(slot, [P, 4, W], F32, "wa_raw%d%d" % (A, a))
+            nc.sync.dma_start(wa_raw[A, a][:], wa_v[a, :, :, A * W:(A + 1) * W])
 
-        def load_g(A, t):
-            g_win[A, t] = big_tile(F32, "g_win%d%d" % (A, t))
+        def load_g(slot, A, t):
+            g_win[A, t] = slot_tile(slot, [P, T], F32, "g_win%d%d" % (A, t))
             nc.sync.dma_start(g_win[A, t][:], gT_v[A, t])
 
-        load_wa(0, 0)
-        load_wa(0, 1)
-        load_g(0, 0)
-        load_g(0, 1)
-        load_wa(1, 0)
-        load_g(0, 2)
-        load_wa(1, 1)
-        load_g(0, 3)
+        nc.sync.dma_start(idx2[:], offs2)
+        nc.sync.dma_start(wb_raw[:], wb_words[0].bitcast(I32))
+        load_plane(wb_sc_raw, wb_scales[0])
+        load_plane(v2_sc_win, tab2_scales[0])
+        v2_win = load_words(0, tab2_words[0], "v2_win")
+        nc.sync.dma_start(idx[:], offs)
         for q in range(4):
-            nc.sync.dma_start(wf_sc[32 * q:32 * q + 8, :], wf_scales[:, 4 * q:4 * q + 4, :].bitcast(I32))
-        with nc.allow_non_contiguous_dma(reason="one bias value a partition"):
-            nc.sync.dma_start(bias_t[:], bias.rearrange("(c p) -> p c", p=P))
-        for t in range(4):
-            load_g(1, t)
-        nc.sync.dma_start(wf_codes[:], wf_words.rearrange("a p e i -> p a (e i)").bitcast(I32))
+            nc.sync.dma_start(v_sc_win[32 * q:32 * q + 8, :], tab_scales[:, 4 * q:4 * q + 4, :].bitcast(I32))
+        nc.scalar.activation(warm[:], one[:], ACT.Abs_reciprocal_sqrt, bias=one[:])
+        v_win = [load_words(1 + a, tab_words[a], "v_win%d" % a) for a in range(2)]
+        load_wa(5, 0, 0)
+        load_wa(7, 0, 1)
+        load_g(3, 0, 0)
+        load_g(4, 0, 1)
+        load_g(6, 0, 2)
+        load_g(8, 0, 3)
+        load_g(9, 1, 0)
 
         def cols(half):
             return slice(half * W, (half + 1) * W)
@@ -133,18 +118,16 @@ def tile_list_regime_damped_signals_kernel(
             nc.vector.tensor_copy(v2_codes[:, cols(half)], v2_win[:].bitcast(U32).indirect(part(idx2, half)))
             nc.vector.tensor_copy(v2_sc[:, cols(half)], v2_sc_win[:].bitcast(U8).indirect(part(idx2, half)))
 
-        gather_regimes(0)
-        permute_wb(0)
-        gather_regimes(1)
-        permute_wb(1)
+        damp = {}
 
-        def damping(A, half):
-            d = damp[2 * A + half]
+        def damping(u, slot):
+            A, half = divmod(u, 2)
+            d = damp[u] = slot_tile(slot, [P, 4, W], F32, "damp%d" % u)
             for t in range(4):
-                u = 4 * A + t
+                c = 4 * A + t
                 b_ps = psum.tile([P, W], F32, name="b_ps", tag="x")
                 nc.tensor.matmul_mx(
-                    b_ps[:], lhsT=wb_codes[:, 256 * u:256 * (u + 1)].bitcast(FP4X4), lhsT_scale=wb_sc[:, P * u:P * (u + 1)],
+                    b_ps[:], lhsT=wb_codes[:, 256 * c:256 * (c + 1)].bitcast(FP4X4), lhsT_scale=wb_sc[:, P * c:P * (c + 1)],
                     rhs=v2_codes[:, cols(half)].bitcast(FP8X4), rhs_scale=v2_sc[:, cols(half)], start=True, stop=True)
                 nc.scalar.activation(d[:, t, :], b_ps[:], ACT.Abs)
             for t in (0, 2):
@@ -152,29 +135,36 @@ def tile_list_regime_damped_signals_kernel(
             for t in (0, 2):
                 nc.scalar.activation(d[:, t:t + 2, :], d[:, t:t + 2, :], ACT.Square)
 
-        def cast_wa(A):
-            tiles = []
+        grouped = {}
+
+        def cast_wa(A, on_pool):
             for a in range(2):
-                grouped = work.tile([P, 4 * W], BF16, name="wa_grouped", align_bytes=64, bufs=3)
-                dst = grouped[:].rearrange("p (t m j) -> p m t j", t=4, j=4)
-                src = wa_raw[A, a][:].rearrange("p (j m t) -> p m t j", j=4, t=4)
-                if CAST_ON_POOL:
+                grouped[A, a] = work.tile([P, 4 * W], BF16, name="wa_grouped", align_bytes=64)
+                dst = grouped[A, a][:].rearrange("p (t m j) -> p m t j", t=4, j=4)
+                src = wa_raw[A, a][:].rearrange("p j (m t) -> p m t j", t=4)
+                if on_pool:
                     nc.gpsimd.tensor_scalar(dst, src, 1.0, 0.0, ALU.mult, ALU.add)
                 else:
                     nc.scalar.copy(dst, src)
-                tiles.append(grouped)
-            return tiles
 
-        def quantise_wa(A, tiles):
+        def quantise_wa(A):
             for a in range(2):
-                nc.vector.quantize_mx(wa_codes[:, 2 * A + a, :].bitcast(FP8X4), wa_sc[:, 2 * A + a, :], tiles[a][:])
+                nc.vector.quantize_mx(wa_codes[:, 2 * A + a, :].bitcast(FP8X4), wa_sc[:, 2 * A + a, :], grouped[A, a][:])
 
-        def gather_carry(u, t, j0=0, j1=W):
-            base = (u % 2) * W
-            nc.vector.tensor_copy(carry[u][:, t, j0:j1], g_win[u // 2, t][:].indirect(idx[:, (base + j0) // 16:(base + j1) // 16]))
+        carry = {}
 
-        def gather_carry01(t):
-            nc.vector.tensor_copy(carry01[:, t, :], g_win[0, t][:].indirect(idx[:]))
+        def gather_carry_pass0():
+            both = keep.tile([P, 4, S], F32, name="carry01")
+            for t in range(4):
+                nc.vector.tensor_copy(both[:, t, :], g_win[0, t][:].indirect(idx[:]))
+            carry[0] = both[:, :, cols(0)]
+            carry[1] = both[:, :, cols(1)]
+
+        def gather_carry(u, slot):
+            tile = slot_tile(slot, [P, 4, W], F32, "carry%d" % u)
+            carry[u] = tile[:]
+            for t in range(4):
+                nc.vector.tensor_copy(carry[u][:, t, :], g_win[u // 2, t][:].indirect(part(idx, u % 2)))
 
         a_ps = {}
 
@@ -189,21 +179,31 @@ def tile_list_regime_damped_signals_kernel(
                         rhs=v_codes[:, a, cols(half)].bitcast(FP8X4), rhs_scale=v_sc[4 * a:P, cols(half)],
                         start=(a == 0), stop=(a == 1))
 
-        def damped(u, t):
-            nc.vector.tensor_tensor(damped_t[u][:, t, :], a_ps[u, t][:], damp[u][:, t, :], ALU.mult)
+        damped = {}
+
+        def damp_loadings(u, slot):
+            damped[u] = slot_tile(slot, [P, 4, W], F32, "damped%d" % u)
+            for t in range(4):
+                nc.vector.tensor_tensor(damped[u][:, t, :], a_ps[u, t][:], damp[u][:, t, :], ALU.mult)
 
         h_bf16 = {}
 
-        def exposures(u, eng, c0, c1):
-            if u not in h_bf16:
-                h_bf16[u] = work.tile([P, 4 * W], BF16, name="h_bf16", align_bytes=64)
+        def exposures(u, eng, pieces):
+            h_bf16[u] = work.tile([P, 4 * W], BF16, name="h_bf16", align_bytes=64, bufs=4)
             dst = h_bf16[u][:].rearrange("p (c i t) -> p c t i", i=4, t=4)
-            q = damped_t[u][:].rearrange("p t (c i) -> p c t i", i=4)
+            q = damped[u][:].rearrange("p t (c i) -> p c t i", i=4)
             g = carry[u].rearrange("p t (c i) -> p c t i", i=4)
-            eng.tensor_tensor(dst[:, c0:c1], q[:, c0:c1], g[:, c0:c1], ALU.add)
+            n = P // pieces
+            for c0 in range(0, P, n):
+                eng.tensor_tensor(dst[:, c0:c0 + n], q[:, c0:c0 + n], g[:, c0:c0 + n], ALU.add)
 
-        def quantise_h(u, j0, j1):
-            nc.vector.quantize_mx(h_codes[:, u, j0:j1].bitcast(FP8X4), h_sc[:, u, j0:j1], h_bf16[u][:, 4 * j0:4 * j1])
+        h_codes = {}
+
+        def quantise_h(u, slot, pieces):
+            h_codes[u] = slot_tile(slot, [P, W], U32, "h_codes%d" % u)
+            n = W // pieces
+            for j0 in range(0, W, n):
+                nc.vector.quantize_mx(h_codes[u][:, j0:j0 + n].bitcast(FP8X4), h_sc[:, u, j0:j0 + n], h_bf16[u][:, 4 * j0:4 * (j0 + n)])
 
         y_ps = {}
 
@@ -214,72 +214,68 @@ def tile_list_regime_damped_signals_kernel(
                 nc.tensor.matmul_mx(
                     y_ps[half, j0, c][:], lhsT=wf_codes[:, A, P * c:P * (c + 1)].bitcast(FP8X4),
                     lhsT_scale=wf_sc[:].bitcast(U8)[4 * A:P, P * c:P * (c + 1)],
-                    rhs=h_codes[:, 2 * A + half, j0:j1].bitcast(FP8X4), rhs_scale=h_sc[:, 2 * A + half, j0:j1],
+                    rhs=h_codes[2 * A + half][:, j0:j1].bitcast(FP8X4), rhs_scale=h_sc[:, 2 * A + half, j0:j1],
                     start=(A == 0), stop=(A == 1))
 
         def store(half, j0, j1, share):
             for c in range(4):
-                y = work.tile([P, j1 - j0], F32, name="y", bufs=4)
+                y = work.tile([P, j1 - j0], F32, name="y", bufs=12)
                 if share and c % 2 == 1:
                     nc.vector.tensor_scalar(y[:], y_ps[half, j0, c][:], bias_t[:, c:c + 1], None, ALU.add)
                 else:
                     nc.scalar.activation(y[:], y_ps[half, j0, c][:], ACT.Identity, bias=bias_t[:, c:c + 1])
                 nc.sync.dma_start(out[P * c:P * (c + 1), half * W + j0:half * W + j1], y[:])
 
-        V = nc.vector
-        G = nc.gpsimd
-        damping(0, 0)
-        damping(0, 1)
-        damping(1, 0)
-        damping(1, 1)
+        permute_wb(0)
+        permute_wb(1)
+        gather_regimes(0)
+        gather_regimes(1)
+        load_wa(0, 1, 0)
+        damping(0, 10)
+        damping(1, 11)
+        damping(2, 12)
         nc.vector.tensor_copy(v_sc[:], v_sc_win[:].bitcast(U8).indirect(idx[:]))
         for a in range(2):
             nc.vector.tensor_copy(v_codes[:, a, :], v_win[a][:].bitcast(U32).indirect(idx[:]))
-        grouped0 = cast_wa(0)
-        quantise_wa(0, grouped0)
+        cast_wa(0, True)
+        load_g(1, 1, 1)
+        load_wa(2, 1, 1)
+        load_g(5, 1, 2)
+        load_g(7, 1, 3)
+        nc.sync.dma_start(wf_codes[:], wf_words.rearrange("a p e i -> p a (e i)").bitcast(I32))
+        for q in range(4):
+            nc.sync.dma_start(wf_sc[32 * q:32 * q + 8, :], wf_scales[:, 4 * q:4 * q + 4, :].bitcast(I32))
+        with nc.allow_non_contiguous_dma(reason="one bias value a partition"):
+            nc.sync.dma_start(bias_t[:], bias.rearrange("(c p) -> p c", p=P))
+        gather_carry_pass0()
+        quantise_wa(0)
         loadings(0)
-        grouped1 = cast_wa(1)
-        for t in range(4):
-            gather_carry01(t)
-        for t in range(4):
-            damped(0, t)
+        damp_loadings(0, 4)
         loadings(1)
-        for c0 in range(0, 128, 32):
-            exposures(0, G, c0, c0 + 32)
-        for t in range(4):
-            damped(1, t)
-        quantise_wa(1, grouped1)
+        exposures(0, nc.gpsimd, 4)
+        damp_loadings(1, 8)
+        exposures(1, nc.gpsimd, 4)
+        cast_wa(1, False)
+        damping(3, 2)
+        gather_carry(2, 11)
+        quantise_wa(1)
         loadings(2)
         loadings(3)
-        for c0 in range(0, 128, 32):
-            exposures(1, G, c0, c0 + 32)
-        for t in range(4):
-            gather_carry(2, t)
-        quantise_h(0, 0, W)
-        for t in range(4):
-            damped(2, t)
+        damp_loadings(2, 3)
+        exposures(2, nc.gpsimd, 4)
+        quantise_h(0, 12, 1)
         signals(0, 0, 0, W, "z")
-        quantise_h(1, 0, W)
-        for c0 in range(0, 128, 32):
-            exposures(2, G, c0, c0 + 32)
-        for t in range(4):
-            damped(3, t)
+        damp_loadings(3, 6)
+        gather_carry(3, 2)
+        quantise_h(1, 9, 1)
         signals(0, 1, 0, 256, "x")
-        carry3 = keep.tile([P, 4, W], F32, name="carry3", tag="damp3")
-        carry[3] = carry3[:]
-        for t in range(4):
-            gather_carry(3, t, 0, 256)
-        quantise_h(2, 0, W)
+        quantise_h(2, 5, 1)
         signals(1, 0, 0, W, "z")
         store(0, 0, W, False)
-        exposures(3, V, 0, 64)
-        for t in range(4):
-            gather_carry(3, t, 256, W)
-        quantise_h(3, 0, 256)
-        signals(1, 1, 0, 256, "x")
         signals(0, 1, 256, W, "z")
-        exposures(3, V, 64, 128)
+        exposures(3, nc.vector, 2)
+        quantise_h(3, 15, 2)
+        signals(1, 1, 0, 256, "x")
         store(1, 0, 256, False)
-        quantise_h(3, 256, W)
         signals(1, 1, 256, W, "z")
         store(1, 256, W, True)

@@ -18,6 +18,7 @@ ALU = mybir.AluOpType
 
 P = 128
 W = 512
+PIECE = 128
 
 
 def tile_list_regime_damped_signals_kernel(
@@ -56,13 +57,9 @@ def tile_list_regime_damped_signals_kernel(
             return slots.tile(shape, dtype, name=name, tag="slot%d" % slot, align_bytes=64)
 
         nc.vector.memset(v_sc_win[:], 0)
+        nc.gpsimd.memset(wb_sc_raw[:], 0)
         nc.gpsimd.memset(one[:], 1.0)
         nc.gpsimd.memset(wf_sc[:], 0)
-
-        def load_plane(tile, rows):
-            for q in range(4):
-                four = rows[4 * q:4 * q + 4, :].bitcast(I32)
-                nc.sync.dma_start(tile[32 * q:32 * q + 32, :], four.unsqueeze(0).broadcast_to([8, 4, four.shape[1]]))
 
         def load_words(slot, words, name):
             win = slot_tile(slot, [P, T], I32, name)
@@ -71,6 +68,7 @@ def tile_list_regime_damped_signals_kernel(
 
         wa_raw = {}
         g_win = {}
+        v_win = {}
         gT_v = gT.rearrange("(A p i) t -> A i p t", A=2, i=4)
         wa_v = wa.rearrange("(a p j) r -> a p j r", a=2, j=4)
 
@@ -83,28 +81,42 @@ def tile_list_regime_damped_signals_kernel(
             nc.sync.dma_start(g_win[A, t][:], gT_v[A, t])
 
         nc.sync.dma_start(idx2[:], offs2)
+        for q in range(4):
+            four = tab2_scales[0, 4 * q:4 * q + 4, :].bitcast(I32)
+            nc.sync.dma_start(v2_sc_win[32 * q:32 * q + 32, :], four.unsqueeze(0).broadcast_to([8, 4, T // 4]))
         nc.sync.dma_start(wb_raw[:], wb_words[0].bitcast(I32))
-        load_plane(wb_sc_raw, wb_scales[0])
-        load_plane(v2_sc_win, tab2_scales[0])
         v2_win = load_words(0, tab2_words[0], "v2_win")
         nc.sync.dma_start(idx[:], offs)
         for q in range(4):
+            nc.sync.dma_start(wb_sc_raw[32 * q:32 * q + 4, :], wb_scales[0, 4 * q:4 * q + 4, :].bitcast(I32))
+        v_win[0] = load_words(1, tab_words[0], "v_win0")
+        for q in range(4):
             nc.sync.dma_start(v_sc_win[32 * q:32 * q + 8, :], tab_scales[:, 4 * q:4 * q + 4, :].bitcast(I32))
         nc.scalar.activation(warm[:], one[:], ACT.Abs_reciprocal_sqrt, bias=one[:])
-        v_win = [load_words(1 + a, tab_words[a], "v_win%d" % a) for a in range(2)]
         load_wa(5, 0, 0)
-        load_wa(7, 0, 1)
+        v_win[1] = load_words(2, tab_words[1], "v_win1")
         load_g(3, 0, 0)
+        load_wa(7, 0, 1)
         load_g(4, 0, 1)
         load_g(6, 0, 2)
+        load_wa(9, 1, 0)
         load_g(8, 0, 3)
-        load_g(9, 1, 0)
+        load_wa(13, 1, 1)
+        load_g(0, 1, 0)
+        load_g(1, 1, 1)
+        load_g(2, 1, 2)
+        load_g(5, 1, 3)
+        nc.sync.dma_start(wf_codes[:], wf_words.rearrange("a p e i -> p a (e i)").bitcast(I32))
+        for q in range(4):
+            nc.sync.dma_start(wf_sc[32 * q:32 * q + 8, :], wf_scales[:, 4 * q:4 * q + 4, :].bitcast(I32))
+        with nc.allow_non_contiguous_dma(reason="one bias value a partition"):
+            nc.sync.dma_start(bias_t[:], bias.rearrange("(c p) -> p c", p=P))
 
         def cols(half):
             return slice(half * W, (half + 1) * W)
 
-        def part(lst, half):
-            return lst[:, half * (W // 16):(half + 1) * (W // 16)]
+        def part(lst, j0, j1):
+            return lst[:, j0 // 16:j1 // 16]
 
         def permute_wb(A):
             nc.vector.tensor_copy(
@@ -113,10 +125,6 @@ def tile_list_regime_damped_signals_kernel(
             nc.vector.tensor_copy(
                 wb_sc[:, cols(A)].rearrange("p (t m) -> p t m", t=4),
                 wb_sc_raw[:].bitcast(U8)[:, cols(A)].rearrange("p (m t) -> p t m", t=4))
-
-        def gather_regimes(half):
-            nc.vector.tensor_copy(v2_codes[:, cols(half)], v2_win[:].bitcast(U32).indirect(part(idx2, half)))
-            nc.vector.tensor_copy(v2_sc[:, cols(half)], v2_sc_win[:].bitcast(U8).indirect(part(idx2, half)))
 
         damp = {}
 
@@ -137,8 +145,8 @@ def tile_list_regime_damped_signals_kernel(
 
         grouped = {}
 
-        def cast_wa(A, on_pool):
-            for a in range(2):
+        def cast_wa(A, a, on_pool):
+            if True:
                 grouped[A, a] = work.tile([P, 4 * W], BF16, name="wa_grouped", align_bytes=64)
                 dst = grouped[A, a][:].rearrange("p (t m j) -> p m t j", t=4, j=4)
                 src = wa_raw[A, a][:].rearrange("p j (m t) -> p m t j", t=4)
@@ -147,31 +155,26 @@ def tile_list_regime_damped_signals_kernel(
                 else:
                     nc.scalar.copy(dst, src)
 
-        def quantise_wa(A):
-            for a in range(2):
+        def quantise_wa(A, a):
+            if True:
                 nc.vector.quantize_mx(wa_codes[:, 2 * A + a, :].bitcast(FP8X4), wa_sc[:, 2 * A + a, :], grouped[A, a][:])
 
         carry = {}
 
-        def gather_carry_pass0():
-            both = keep.tile([P, 4, S], F32, name="carry01")
-            for t in range(4):
-                nc.vector.tensor_copy(both[:, t, :], g_win[0, t][:].indirect(idx[:]))
-            carry[0] = both[:, :, cols(0)]
-            carry[1] = both[:, :, cols(1)]
+        def carry_at(A, j0, j1):
+            if A == 1 and j0 >= W:
+                return damp[2][:, :, j0 - W:j1 - W]
+            return carry[A][:, :, j0:j1]
 
-        def gather_carry(u, slot):
-            tile = slot_tile(slot, [P, 4, W], F32, "carry%d" % u)
-            carry[u] = tile[:]
-            for t in range(4):
-                nc.vector.tensor_copy(carry[u][:, t, :], g_win[u // 2, t][:].indirect(part(idx, u % 2)))
+        def gather_carry(A, t, j0, j1):
+            nc.vector.tensor_copy(carry_at(A, j0, j1)[:, t, :], g_win[A, t][:].indirect(part(idx, j0, j1)))
 
         a_ps = {}
 
         def loadings(u):
             A, half = divmod(u, 2)
             for t in range(4):
-                a_ps[u, t] = psum.tile([P, W], F32, name="a_ps", tag=("x" if u == 3 else "z"))
+                a_ps[u, t] = psum.tile([P, W], F32, name="a_ps", tag="z")
                 for a in range(2):
                     nc.tensor.matmul_mx(
                         a_ps[u, t][:], lhsT=wa_codes[:, 2 * A + a, P * t:P * (t + 1)].bitcast(FP8X4),
@@ -182,100 +185,123 @@ def tile_list_regime_damped_signals_kernel(
         damped = {}
 
         def damp_loadings(u, slot):
-            damped[u] = slot_tile(slot, [P, 4, W], F32, "damped%d" % u)
+            damped[u] = damp[u] if slot is None else slot_tile(slot, [P, 4, W], F32, "damped%d" % u)
             for t in range(4):
                 nc.vector.tensor_tensor(damped[u][:, t, :], a_ps[u, t][:], damp[u][:, t, :], ALU.mult)
 
         h_bf16 = {}
 
-        def exposures(u, eng, pieces):
-            h_bf16[u] = work.tile([P, 4 * W], BF16, name="h_bf16", align_bytes=64, bufs=4)
-            dst = h_bf16[u][:].rearrange("p (c i t) -> p c t i", i=4, t=4)
-            q = damped[u][:].rearrange("p t (c i) -> p c t i", i=4)
-            g = carry[u].rearrange("p t (c i) -> p c t i", i=4)
-            n = P // pieces
-            for c0 in range(0, P, n):
-                eng.tensor_tensor(dst[:, c0:c0 + n], q[:, c0:c0 + n], g[:, c0:c0 + n], ALU.add)
+        def h_at(A, j0, j1):
+            width = 256 if (A == 1 and j0 >= W) else W
+            base = j0 // width * width
+            if (A, base) not in h_bf16:
+                if width == W:
+                    h_bf16[A, base] = work.tile([P, 4 * W], BF16, name="h_bf16", align_bytes=64, bufs=3)
+                else:
+                    h_bf16[A, base] = work.tile([P, 4 * width], BF16, name="h_last", align_bytes=64, bufs=1)
+            return h_bf16[A, base][:, 4 * (j0 - base):4 * (j1 - base)]
 
-        h_codes = {}
+        def exposures(A, j0, j1, eng):
+            half, i0 = divmod(j0, W)
+            u = 2 * A + half
+            i1 = i0 + j1 - j0
+            dst = h_at(A, j0, j1).rearrange("p (c i t) -> p c t i", i=4, t=4)
+            q = damped[u][:, :, i0:i1].rearrange("p t (c i) -> p c t i", i=4)
+            g = carry_at(A, j0, j1).rearrange("p t (c i) -> p c t i", i=4)
+            eng.tensor_tensor(dst, q, g, ALU.add)
 
-        def quantise_h(u, slot, pieces):
-            h_codes[u] = slot_tile(slot, [P, W], U32, "h_codes%d" % u)
-            n = W // pieces
-            for j0 in range(0, W, n):
-                nc.vector.quantize_mx(h_codes[u][:, j0:j0 + n].bitcast(FP8X4), h_sc[:, u, j0:j0 + n], h_bf16[u][:, 4 * j0:4 * (j0 + n)])
+        h_codes = keep.tile([P, 4, W], U32, name="h_codes", align_bytes=64)
+
+        def quantise_h(A, j0, j1):
+            half, i0 = divmod(j0, W)
+            u = 2 * A + half
+            i1 = i0 + j1 - j0
+            nc.vector.quantize_mx(h_codes[:, u, i0:i1].bitcast(FP8X4), h_sc[:, u, i0:i1], h_at(A, j0, j1))
 
         y_ps = {}
 
-        def signals(A, half, j0, j1, tag):
+        def signals(A, j0, j1, tag):
+            half, i0 = divmod(j0, W)
+            u = 2 * A + half
+            i1 = i0 + j1 - j0
             for c in range(4):
                 if A == 0:
-                    y_ps[half, j0, c] = psum.tile([P, j1 - j0], F32, name="y_ps", tag=tag)
+                    y_ps[j0, c] = psum.tile([P, j1 - j0], F32, name="y_ps", tag=tag)
                 nc.tensor.matmul_mx(
-                    y_ps[half, j0, c][:], lhsT=wf_codes[:, A, P * c:P * (c + 1)].bitcast(FP8X4),
+                    y_ps[j0, c][:], lhsT=wf_codes[:, A, P * c:P * (c + 1)].bitcast(FP8X4),
                     lhsT_scale=wf_sc[:].bitcast(U8)[4 * A:P, P * c:P * (c + 1)],
-                    rhs=h_codes[2 * A + half][:, j0:j1].bitcast(FP8X4), rhs_scale=h_sc[:, 2 * A + half, j0:j1],
+                    rhs=h_codes[:, u, i0:i1].bitcast(FP8X4), rhs_scale=h_sc[:, u, i0:i1],
                     start=(A == 0), stop=(A == 1))
 
-        def store(half, j0, j1, share):
+        def store(j0, j1, share):
             for c in range(4):
-                y = work.tile([P, j1 - j0], F32, name="y", bufs=12)
+                y = work.tile([P, j1 - j0], F32, name="y", bufs=8)
                 if share and c % 2 == 1:
-                    nc.vector.tensor_scalar(y[:], y_ps[half, j0, c][:], bias_t[:, c:c + 1], None, ALU.add)
+                    nc.vector.tensor_scalar(y[:], y_ps[j0, c][:], bias_t[:, c:c + 1], None, ALU.add)
                 else:
-                    nc.scalar.activation(y[:], y_ps[half, j0, c][:], ACT.Identity, bias=bias_t[:, c:c + 1])
-                nc.sync.dma_start(out[P * c:P * (c + 1), half * W + j0:half * W + j1], y[:])
+                    nc.scalar.activation(y[:], y_ps[j0, c][:], ACT.Identity, bias=bias_t[:, c:c + 1])
+                nc.sync.dma_start(out[P * c:P * (c + 1), j0:j1], y[:])
 
-        permute_wb(0)
-        permute_wb(1)
-        gather_regimes(0)
-        gather_regimes(1)
-        load_wa(0, 1, 0)
+        nc.vector.tensor_copy(v2_sc[:], v2_sc_win[:].bitcast(U8).indirect(idx2[:]))
+        for half in range(2):
+            permute_wb(half)
+            nc.vector.tensor_copy(v2_codes[:, cols(half)], v2_win[:].bitcast(U32).indirect(part(idx2, half * W, (half + 1) * W)))
         damping(0, 10)
         damping(1, 11)
-        damping(2, 12)
         nc.vector.tensor_copy(v_sc[:], v_sc_win[:].bitcast(U8).indirect(idx[:]))
         for a in range(2):
             nc.vector.tensor_copy(v_codes[:, a, :], v_win[a][:].bitcast(U32).indirect(idx[:]))
-        cast_wa(0, True)
-        load_g(1, 1, 1)
-        load_wa(2, 1, 1)
-        load_g(5, 1, 2)
-        load_g(7, 1, 3)
-        nc.sync.dma_start(wf_codes[:], wf_words.rearrange("a p e i -> p a (e i)").bitcast(I32))
-        for q in range(4):
-            nc.sync.dma_start(wf_sc[32 * q:32 * q + 8, :], wf_scales[:, 4 * q:4 * q + 4, :].bitcast(I32))
-        with nc.allow_non_contiguous_dma(reason="one bias value a partition"):
-            nc.sync.dma_start(bias_t[:], bias.rearrange("(c p) -> p c", p=P))
-        gather_carry_pass0()
-        quantise_wa(0)
+        for a in range(2):
+            cast_wa(0, a, True)
+            quantise_wa(0, a)
+        carry[0] = keep.tile([P, 4, S], F32, name="carry0")
+        for t in range(3):
+            gather_carry(0, t, 0, S)
         loadings(0)
-        damp_loadings(0, 4)
+        damp_loadings(0, None)
+        gather_carry(0, 3, 0, W)
+        gather_carry(0, 3, W, S)
         loadings(1)
-        exposures(0, nc.gpsimd, 4)
-        damp_loadings(1, 8)
-        exposures(1, nc.gpsimd, 4)
-        cast_wa(1, False)
-        damping(3, 2)
-        gather_carry(2, 11)
-        quantise_wa(1)
+        cast_wa(1, 0, True)
+        for j0 in range(0, W, PIECE):
+            exposures(0, j0, j0 + PIECE, nc.gpsimd)
+        damp_loadings(1, None)
+        for j0 in range(W, S, PIECE):
+            exposures(0, j0, j0 + PIECE, nc.gpsimd)
+        cast_wa(1, 1, False)
+        damping(2, 12)
+        damping(3, 14)
+        quantise_wa(1, 0)
+        quantise_wa(1, 1)
         loadings(2)
+        damp_loadings(2, None)
         loadings(3)
-        damp_loadings(2, 3)
-        exposures(2, nc.gpsimd, 4)
-        quantise_h(0, 12, 1)
-        signals(0, 0, 0, W, "z")
-        damp_loadings(3, 6)
-        gather_carry(3, 2)
-        quantise_h(1, 9, 1)
-        signals(0, 1, 0, 256, "x")
-        quantise_h(2, 5, 1)
-        signals(1, 0, 0, W, "z")
-        store(0, 0, W, False)
-        signals(0, 1, 256, W, "z")
-        exposures(3, nc.vector, 2)
-        quantise_h(3, 15, 2)
-        signals(1, 1, 0, 256, "x")
-        store(1, 0, 256, False)
-        signals(1, 1, 256, W, "z")
-        store(1, 256, W, True)
+        carry[1] = keep.tile([P, 4, W], F32, name="carry1")
+        for t in range(3):
+            gather_carry(1, t, 0, W)
+        quantise_h(0, 0, W)
+        quantise_h(0, W, S)
+        signals(0, 0, W, "x")
+        for j0 in range(0, W, 256):
+            gather_carry(1, 3, j0, j0 + 256)
+        for j0 in range(0, W, PIECE):
+            exposures(1, j0, j0 + PIECE, nc.gpsimd)
+        damp_loadings(3, None)
+        signals(0, W, W + 256, "z")
+        for t in range(4):
+            gather_carry(1, t, W, W + 256)
+        quantise_h(1, 0, W)
+        signals(1, 0, W, "x")
+        store(0, W, False)
+        signals(0, W + 256, S, "x")
+        for j0 in range(W, W + 256, PIECE):
+            exposures(1, j0, j0 + PIECE, nc.gpsimd)
+        for t in range(4):
+            gather_carry(1, t, W + 256, S)
+        quantise_h(1, W, W + 256)
+        signals(1, W, W + 256, "z")
+        store(W, W + 256, False)
+        exposures(1, W + 256, S, nc.vector)
+        quantise_h(1, W + 256, S)
+        signals(1, W + 256, S, "x")
+        store(W + 256, S, True)

@@ -41,7 +41,6 @@ def tile_list_regime_damped_signals_kernel(
         wb_raw = keep.tile([P, H // 2], I32, name="wb_raw", align_bytes=64)
         wb_codes = keep.tile([P, 2 * H], U8, name="wb_codes", align_bytes=64)
         wb_sc = keep.tile([P, H], U8, name="wb_sc", align_bytes=64)
-        wf_codes = keep.tile([P, 2, N], I32, name="wf_codes", align_bytes=64)
         bias_t = keep.tile([P, 4], F32, name="bias_t")
         one = keep.tile([P, 1], F32, name="one")
         warm = keep.tile([P, 1], F32, name="warm")
@@ -49,7 +48,7 @@ def tile_list_regime_damped_signals_kernel(
         v_sc = keep.tile([P, S], U8, name="v_sc", align_bytes=64)
         v2_codes = keep.tile([P, S], U32, name="v2_codes", align_bytes=64)
         v2_sc = keep.tile([P, S], U8, name="v2_sc", align_bytes=64)
-        wa_codes = keep.tile([P, 4, W], U32, name="wa_codes", align_bytes=64)
+        wa_codes = {}
         wa_sc = keep.tile([P, 4, W], U8, name="wa_sc", align_bytes=64)
         h_sc = keep.tile([P, 4, W], U8, name="h_sc", align_bytes=64)
 
@@ -104,9 +103,8 @@ def tile_list_regime_damped_signals_kernel(
         load_wa(13, 1, 1)
         load_g(0, 1, 0)
         load_g(1, 1, 1)
-        load_g(2, 1, 2)
-        load_g(5, 1, 3)
-        nc.sync.dma_start(wf_codes[:], wf_words.rearrange("a p e i -> p a (e i)").bitcast(I32))
+        load_g(14, 1, 2)
+        load_g(3, 1, 3)
         for q in range(4):
             nc.sync.dma_start(wf_sc[32 * q:32 * q + 8, :], wf_scales[:, 4 * q:4 * q + 4, :].bitcast(I32))
         with nc.allow_non_contiguous_dma(reason="one bias value a partition"):
@@ -128,20 +126,24 @@ def tile_list_regime_damped_signals_kernel(
 
         damp = {}
 
-        def damping(u, slot):
+        def damping(u, parts):
             A, half = divmod(u, 2)
-            d = damp[u] = slot_tile(slot, [P, 4, W], F32, "damp%d" % u)
+            for i0, i1, slot in parts:
+                damp[u, i0] = slot_tile(slot, [P, 4, i1 - i0], F32, "damp%d_%d" % (u, i0))
             for t in range(4):
                 c = 4 * A + t
-                b_ps = psum.tile([P, W], F32, name="b_ps", tag="x")
+                b_ps = psum.tile([P, W], F32, name="b_ps", tag=("z" if u == 3 else "x"))
                 nc.tensor.matmul_mx(
                     b_ps[:], lhsT=wb_codes[:, 256 * c:256 * (c + 1)].bitcast(FP4X4), lhsT_scale=wb_sc[:, P * c:P * (c + 1)],
                     rhs=v2_codes[:, cols(half)].bitcast(FP8X4), rhs_scale=v2_sc[:, cols(half)], start=True, stop=True)
-                nc.scalar.activation(d[:, t, :], b_ps[:], ACT.Abs)
-            for t in (0, 2):
-                nc.scalar.activation(d[:, t:t + 2, :], d[:, t:t + 2, :], ACT.Abs_reciprocal_sqrt, bias=one[:])
-            for t in (0, 2):
-                nc.scalar.activation(d[:, t:t + 2, :], d[:, t:t + 2, :], ACT.Square)
+                for i0, i1, slot in parts:
+                    nc.scalar.activation(damp[u, i0][:, t, :], b_ps[:, i0:i1], ACT.Abs)
+            step = 2 * len(parts)
+            runs = [damp[u, i0][:, t:t + step, :] for i0, i1, slot in parts for t in range(0, 4, step)]
+            for d in runs:
+                nc.scalar.activation(d, d, ACT.Abs_reciprocal_sqrt, bias=one[:])
+            for d in runs:
+                nc.scalar.activation(d, d, ACT.Square)
 
         grouped = {}
 
@@ -157,14 +159,14 @@ def tile_list_regime_damped_signals_kernel(
 
         def quantise_wa(A, a):
             if True:
-                nc.vector.quantize_mx(wa_codes[:, 2 * A + a, :].bitcast(FP8X4), wa_sc[:, 2 * A + a, :], grouped[A, a][:])
+                wa_codes[A, a] = slot_tile({(0, 0): 2, (0, 1): 4, (1, 0): 31, (1, 1): 32}[A, a], [P, W], U32, "wa_codes%d%d" % (A, a))
+                nc.vector.quantize_mx(wa_codes[A, a][:].bitcast(FP8X4), wa_sc[:, 2 * A + a, :], grouped[A, a][:])
 
         carry = {}
 
         def carry_at(A, j0, j1):
-            if A == 1 and j0 >= W:
-                return damp[2][:, :, j0 - W:j1 - W]
-            return carry[A][:, :, j0:j1]
+            base = max(b for (a, b) in carry if a == A and b <= j0)
+            return carry[A, base][:, :, j0 - base:j1 - base]
 
         def gather_carry(A, t, j0, j1):
             nc.vector.tensor_copy(carry_at(A, j0, j1)[:, t, :], g_win[A, t][:].indirect(part(idx, j0, j1)))
@@ -174,20 +176,23 @@ def tile_list_regime_damped_signals_kernel(
         def loadings(u):
             A, half = divmod(u, 2)
             for t in range(4):
-                a_ps[u, t] = psum.tile([P, W], F32, name="a_ps", tag="z")
+                a_ps[u, t] = psum.tile([P, W], F32, name="a_ps", tag=("x" if u in (1, 2) else "z"))
                 for a in range(2):
                     nc.tensor.matmul_mx(
-                        a_ps[u, t][:], lhsT=wa_codes[:, 2 * A + a, P * t:P * (t + 1)].bitcast(FP8X4),
+                        a_ps[u, t][:], lhsT=wa_codes[A, a][:, P * t:P * (t + 1)].bitcast(FP8X4),
                         lhsT_scale=wa_sc[:, 2 * A + a, P * t:P * (t + 1)],
                         rhs=v_codes[:, a, cols(half)].bitcast(FP8X4), rhs_scale=v_sc[4 * a:P, cols(half)],
                         start=(a == 0), stop=(a == 1))
 
         damped = {}
 
-        def damp_loadings(u, slot):
-            damped[u] = damp[u] if slot is None else slot_tile(slot, [P, 4, W], F32, "damped%d" % u)
+        def damp_loadings(u, parts):
+            for i0, i1, slot in parts:
+                damped[u, i0] = slot_tile(slot, [P, 4, i1 - i0], F32, "damped%d_%d" % (u, i0))
             for t in range(4):
-                nc.vector.tensor_tensor(damped[u][:, t, :], a_ps[u, t][:], damp[u][:, t, :], ALU.mult)
+                for i0, i1, slot in parts:
+                    base = max(b for (v, b) in damp if v == u and b <= i0)
+                    nc.vector.tensor_tensor(damped[u, i0][:, t, :], a_ps[u, t][:, i0:i1], damp[u, base][:, t, i0 - base:i1 - base], ALU.mult)
 
         h_bf16 = {}
 
@@ -196,7 +201,13 @@ def tile_list_regime_damped_signals_kernel(
             base = j0 // width * width
             if (A, base) not in h_bf16:
                 if width == W:
-                    h_bf16[A, base] = work.tile([P, 4 * W], BF16, name="h_bf16", align_bytes=64, bufs=3)
+                    if (A, base) == (0, 0):
+                        h_bf16[A, base] = keep.tile([P, 4 * W], BF16, name="h_first", align_bytes=64)
+                    else:
+                        pair = keep.tile([P, 2, 4 * W], BF16, name="h_pair", align_bytes=64)
+                        h_bf16[0, W] = pair[:, 0, :]
+                        h_bf16[1, 0] = pair[:, 1, :]
+                        h_bf16["pair"] = pair
                 else:
                     h_bf16[A, base] = work.tile([P, 4 * width], BF16, name="h_last", align_bytes=64, bufs=1)
             return h_bf16[A, base][:, 4 * (j0 - base):4 * (j1 - base)]
@@ -206,17 +217,28 @@ def tile_list_regime_damped_signals_kernel(
             u = 2 * A + half
             i1 = i0 + j1 - j0
             dst = h_at(A, j0, j1).rearrange("p (c i t) -> p c t i", i=4, t=4)
-            q = damped[u][:, :, i0:i1].rearrange("p t (c i) -> p c t i", i=4)
+            base = max(b for (v, b) in damped if v == u and b <= i0)
+            q = damped[u, base][:, :, i0 - base:i1 - base].rearrange("p t (c i) -> p c t i", i=4)
             g = carry_at(A, j0, j1).rearrange("p t (c i) -> p c t i", i=4)
             eng.tensor_tensor(dst, q, g, ALU.add)
 
-        h_codes = keep.tile([P, 4, W], U32, name="h_codes", align_bytes=64)
+        h_codes = {}
 
-        def quantise_h(A, j0, j1):
+        def quantise_h(A, j0, j1, slot):
             half, i0 = divmod(j0, W)
             u = 2 * A + half
             i1 = i0 + j1 - j0
-            nc.vector.quantize_mx(h_codes[:, u, i0:i1].bitcast(FP8X4), h_sc[:, u, i0:i1], h_at(A, j0, j1))
+            if True:
+                h_codes[A, j0] = slot_tile(slot, [P, j1 - j0], U32, "h_codes%d_%d" % (A, j0))[:]
+            nc.vector.quantize_mx(h_codes[A, j0].bitcast(FP8X4), h_sc[:, u, i0:i1], h_at(A, j0, j1))
+
+        def quantise_pair(slot):
+            codes = slot_tile(slot, [P, 2, W], U32, "h_codes_pair")
+            h_codes[0, W] = codes[:, 0, :]
+            h_codes[1, 0] = codes[:, 1, :]
+            nc.vector.quantize_mx(
+                codes[:].rearrange("p u j -> p (u j)").bitcast(FP8X4), h_sc[:, 1:3, :].rearrange("p u j -> p (u j)"),
+                h_bf16["pair"][:].rearrange("p u j -> p (u j)"))
 
         y_ps = {}
 
@@ -224,13 +246,14 @@ def tile_list_regime_damped_signals_kernel(
             half, i0 = divmod(j0, W)
             u = 2 * A + half
             i1 = i0 + j1 - j0
+            base = max(b for (a, b) in h_codes if a == A and b <= j0)
             for c in range(4):
                 if A == 0:
                     y_ps[j0, c] = psum.tile([P, j1 - j0], F32, name="y_ps", tag=tag)
                 nc.tensor.matmul_mx(
                     y_ps[j0, c][:], lhsT=wf_codes[:, A, P * c:P * (c + 1)].bitcast(FP8X4),
                     lhsT_scale=wf_sc[:].bitcast(U8)[4 * A:P, P * c:P * (c + 1)],
-                    rhs=h_codes[:, u, i0:i1].bitcast(FP8X4), rhs_scale=h_sc[:, u, i0:i1],
+                    rhs=h_codes[A, base][:, j0 - base:j1 - base].bitcast(FP8X4), rhs_scale=h_sc[:, u, i0:i1],
                     start=(A == 0), stop=(A == 1))
 
         def store(j0, j1, share):
@@ -246,62 +269,70 @@ def tile_list_regime_damped_signals_kernel(
         for half in range(2):
             permute_wb(half)
             nc.vector.tensor_copy(v2_codes[:, cols(half)], v2_win[:].bitcast(U32).indirect(part(idx2, half * W, (half + 1) * W)))
-        damping(0, 10)
-        damping(1, 11)
+        damping(0, [(0, W, 10)])
+        damping(1, [(0, W, 11)])
+        damping(2, [(0, P, 12), (P, W, 15)])
         nc.vector.tensor_copy(v_sc[:], v_sc_win[:].bitcast(U8).indirect(idx[:]))
         for a in range(2):
             nc.vector.tensor_copy(v_codes[:, a, :], v_win[a][:].bitcast(U32).indirect(idx[:]))
         for a in range(2):
             cast_wa(0, a, True)
             quantise_wa(0, a)
-        carry[0] = keep.tile([P, 4, S], F32, name="carry0")
+        wf_codes = slot_tile(4, [P, 2, N], I32, "wf_codes")
+        nc.sync.dma_start(wf_codes[:], wf_words.rearrange("a p e i -> p a (e i)").bitcast(I32))
+        carry[0, 0] = keep.tile([P, 4, S], F32, name="carry0")
         for t in range(3):
             gather_carry(0, t, 0, S)
         loadings(0)
-        damp_loadings(0, None)
+        damp_loadings(0, [(0, W, 6)])
         gather_carry(0, 3, 0, W)
         gather_carry(0, 3, W, S)
         loadings(1)
         cast_wa(1, 0, True)
         for j0 in range(0, W, PIECE):
             exposures(0, j0, j0 + PIECE, nc.gpsimd)
-        damp_loadings(1, None)
+        damp_loadings(1, [(0, W, 8)])
         for j0 in range(W, S, PIECE):
             exposures(0, j0, j0 + PIECE, nc.gpsimd)
         cast_wa(1, 1, False)
-        damping(2, 12)
-        damping(3, 14)
+        damping(3, [(0, 256, 13), (256, W, 15)])
         quantise_wa(1, 0)
         quantise_wa(1, 1)
         loadings(2)
-        damp_loadings(2, None)
+        damp_loadings(2, [(0, P, 5), (P, W, 7)])
         loadings(3)
-        carry[1] = keep.tile([P, 4, W], F32, name="carry1")
-        for t in range(3):
-            gather_carry(1, t, 0, W)
-        quantise_h(0, 0, W)
-        quantise_h(0, W, S)
-        signals(0, 0, W, "x")
-        for j0 in range(0, W, 256):
-            gather_carry(1, 3, j0, j0 + 256)
-        for j0 in range(0, W, PIECE):
-            exposures(1, j0, j0 + PIECE, nc.gpsimd)
-        damp_loadings(3, None)
-        signals(0, W, W + 256, "z")
+        for q in range(2):
+            carry[1, 256 * q] = slot_tile(16 + q, [P, 4, 256], F32, "carry1_%d" % q)
         for t in range(4):
+            for j0 in range(0, W, 256):
+                gather_carry(1, t, j0, j0 + 256)
+        quantise_h(0, 0, W, 12)
+        signals(0, 0, W, "x")
+        exposures(1, 0, P, nc.vector)
+        for j0, j1 in ((128, 192), (192, 256), (256, 384), (384, 512)):
+            exposures(1, j0, j1, nc.gpsimd)
+        damp_loadings(3, [(0, 256, 5)])
+        late = slot_tile(13, [P, 2, 4, 256], F32, "carry_late")
+        carry[1, W] = late[:, 0]
+        carry[1, W + 256] = late[:, 1]
+        gather_carry(1, 0, W, W + 256)
+        gather_carry(1, 0, W + 256, S)
+        for t in range(1, 4):
             gather_carry(1, t, W, W + 256)
-        quantise_h(1, 0, W)
+        quantise_pair(0)
         signals(1, 0, W, "x")
         store(0, W, False)
-        signals(0, W + 256, S, "x")
         for j0 in range(W, W + 256, PIECE):
             exposures(1, j0, j0 + PIECE, nc.gpsimd)
-        for t in range(4):
+        damp_loadings(3, [(256, W, 16)])
+        signals(0, W, W + 256, "z")
+        signals(0, W + 256, S, "x")
+        for t in range(1, 4):
             gather_carry(1, t, W + 256, S)
-        quantise_h(1, W, W + 256)
+        quantise_h(1, W, W + 256, 3)
         signals(1, W, W + 256, "z")
         store(W, W + 256, False)
         exposures(1, W + 256, S, nc.vector)
-        quantise_h(1, W + 256, S)
+        quantise_h(1, W + 256, S, 9)
         signals(1, W + 256, S, "x")
         store(W + 256, S, True)

@@ -120,7 +120,7 @@ def tile_list_regime_damped_signals_kernel(
             nc.vector.tensor_copy(
                 wb_codes[:].bitcast(U16)[:, cols(A)].rearrange("p (t m) -> p t m", t=4),
                 wb_raw[:].bitcast(U16)[:, cols(A)].rearrange("p (m t) -> p t m", t=4))
-            nc.vector.tensor_copy(
+            nc.gpsimd.tensor_copy(
                 wb_sc[:, cols(A)].rearrange("p (t m) -> p t m", t=4),
                 wb_sc_raw[:].bitcast(U8)[:, cols(A)].rearrange("p (m t) -> p t m", t=4))
 

@@ -18,7 +18,6 @@ ALU = mybir.AluOpType
 
 P = 128
 W = 512
-PIECE = 128
 
 
 def tile_list_regime_damped_signals_kernel(
@@ -79,6 +78,11 @@ def tile_list_regime_damped_signals_kernel(
             g_win[A, t] = slot_tile(slot, [P, T], F32, "g_win%d%d" % (A, t))
             nc.sync.dma_start(g_win[A, t][:], gT_v[A, t])
 
+        def load_plane(a):
+            for q in range(4):
+                p0 = 32 * q + 4 * (a + 1)
+                nc.sync.dma_start(v_sc_win[p0:p0 + 4, :], tab_scales[a, 4 * q:4 * q + 4, :].bitcast(I32))
+
         nc.sync.dma_start(idx2[:], offs2)
         for q in range(4):
             four = tab2_scales[0, 4 * q:4 * q + 4, :].bitcast(I32)
@@ -89,10 +93,10 @@ def tile_list_regime_damped_signals_kernel(
         for q in range(4):
             nc.sync.dma_start(wb_sc_raw[32 * q:32 * q + 4, :], wb_scales[0, 4 * q:4 * q + 4, :].bitcast(I32))
         v_win[0] = load_words(1, tab_words[0], "v_win0")
-        for q in range(4):
-            nc.sync.dma_start(v_sc_win[32 * q:32 * q + 8, :], tab_scales[:, 4 * q:4 * q + 4, :].bitcast(I32))
+        load_plane(0)
         nc.scalar.activation(warm[:], one[:], ACT.Abs_reciprocal_sqrt, bias=one[:])
         load_wa(5, 0, 0)
+        load_plane(1)
         v_win[1] = load_words(2, tab_words[1], "v_win1")
         load_g(3, 0, 0)
         load_wa(7, 0, 1)
@@ -177,12 +181,13 @@ def tile_list_regime_damped_signals_kernel(
             A, half = divmod(u, 2)
             for t in range(4):
                 a_ps[u, t] = psum.tile([P, W], F32, name="a_ps", tag=("x" if u in (1, 2) else "z"))
-                for a in range(2):
+                order = (1, 0) if half else (0, 1)
+                for a in order:
                     nc.tensor.matmul_mx(
                         a_ps[u, t][:], lhsT=wa_codes[A, a][:, P * t:P * (t + 1)].bitcast(FP8X4),
                         lhsT_scale=wa_sc[:, 2 * A + a, P * t:P * (t + 1)],
-                        rhs=v_codes[:, a, cols(half)].bitcast(FP8X4), rhs_scale=v_sc[4 * a:P, cols(half)],
-                        start=(a == 0), stop=(a == 1))
+                        rhs=v_codes[:, a, cols(half)].bitcast(FP8X4), rhs_scale=v_sc[4 * (a + 1):P, cols(half)],
+                        start=(a == order[0]), stop=(a == order[1]))
 
         damped = {}
 
@@ -289,11 +294,11 @@ def tile_list_regime_damped_signals_kernel(
         gather_carry(0, 3, W, S)
         loadings(1)
         cast_wa(1, 0, True)
-        for j0 in range(0, W, PIECE):
-            exposures(0, j0, j0 + PIECE, nc.gpsimd)
+        for j0, j1 in ((0, 256), (256, 384), (384, 512)):
+            exposures(0, j0, j1, nc.gpsimd)
         damp_loadings(1, [(0, W, 8)])
-        for j0 in range(W, S, PIECE):
-            exposures(0, j0, j0 + PIECE, nc.gpsimd)
+        for j0, j1 in ((512, 640), (640, 768), (768, 1024)):
+            exposures(0, j0, j1, nc.gpsimd)
         cast_wa(1, 1, False)
         damping(3, [(0, 256, 13), (256, W, 15)])
         quantise_wa(1, 0)
@@ -309,7 +314,7 @@ def tile_list_regime_damped_signals_kernel(
         quantise_h(0, 0, W, 12)
         signals(0, 0, W, "x")
         exposures(1, 0, P, nc.vector)
-        for j0, j1 in ((128, 192), (192, 256), (256, 384), (384, 512)):
+        for j0, j1 in ((128, 192), (192, 256), (256, 512)):
             exposures(1, j0, j1, nc.gpsimd)
         damp_loadings(3, [(0, 256, 5)])
         late = slot_tile(13, [P, 2, 4, 256], F32, "carry_late")
@@ -322,8 +327,7 @@ def tile_list_regime_damped_signals_kernel(
         quantise_pair(0)
         signals(1, 0, W, "x")
         store(0, W, False)
-        for j0 in range(W, W + 256, PIECE):
-            exposures(1, j0, j0 + PIECE, nc.gpsimd)
+        exposures(1, W, W + 256, nc.gpsimd)
         damp_loadings(3, [(256, W, 16)])
         signals(0, W, W + 256, "z")
         signals(0, W + 256, S, "x")

@@ -193,7 +193,8 @@ def tile_list_regime_damped_signals_kernel(
 
         def damp_loadings(u, parts):
             for i0, i1, slot in parts:
-                damped[u, i0] = slot_tile(slot, [P, 4, i1 - i0], F32, "damped%d_%d" % (u, i0))
+                if slot is not None:
+                    damped[u, i0] = slot_tile(slot, [P, 4, i1 - i0], F32, "damped%d_%d" % (u, i0))[:]
             for t in range(4):
                 for i0, i1, slot in parts:
                     base = max(b for (v, b) in damp if v == u and b <= i0)
@@ -209,12 +210,12 @@ def tile_list_regime_damped_signals_kernel(
                     if (A, base) == (0, 0):
                         h_bf16[A, base] = keep.tile([P, 4 * W], BF16, name="h_first", align_bytes=64)
                     else:
-                        pair = keep.tile([P, 2, 4 * W], BF16, name="h_pair", align_bytes=64)
+                        pair = slot_tile(20, [P, 2, 4 * W], BF16, "h_pair")
                         h_bf16[0, W] = pair[:, 0, :]
                         h_bf16[1, 0] = pair[:, 1, :]
                         h_bf16["pair"] = pair
                 else:
-                    h_bf16[A, base] = work.tile([P, 4 * width], BF16, name="h_last", align_bytes=64, bufs=1)
+                    h_bf16[A, base] = slot_tile(20 if base == W else 21, [P, 4 * width], BF16, "h_last%d" % base)
             return h_bf16[A, base][:, 4 * (j0 - base):4 * (j1 - base)]
 
         def exposures(A, j0, j1, eng):
@@ -276,7 +277,7 @@ def tile_list_regime_damped_signals_kernel(
             nc.vector.tensor_copy(v2_codes[:, cols(half)], v2_win[:].bitcast(U32).indirect(part(idx2, half * W, (half + 1) * W)))
         damping(0, [(0, W, 10)])
         damping(1, [(0, W, 11)])
-        damping(2, [(0, P, 12), (P, W, 15)])
+        damping(2, [(0, 32, 12), (32, W, 15)])
         nc.vector.tensor_copy(v_sc[:], v_sc_win[:].bitcast(U8).indirect(idx[:]))
         for a in range(2):
             nc.vector.tensor_copy(v_codes[:, a, :], v_win[a][:].bitcast(U32).indirect(idx[:]))
@@ -304,7 +305,7 @@ def tile_list_regime_damped_signals_kernel(
         quantise_wa(1, 0)
         quantise_wa(1, 1)
         loadings(2)
-        damp_loadings(2, [(0, P, 5), (P, W, 7)])
+        damp_loadings(2, [(0, 32, 5), (32, W, 7)])
         loadings(3)
         for q in range(2):
             carry[1, 256 * q] = slot_tile(16 + q, [P, 4, 256], F32, "carry1_%d" % q)
@@ -313,10 +314,12 @@ def tile_list_regime_damped_signals_kernel(
                 gather_carry(1, t, j0, j0 + 256)
         quantise_h(0, 0, W, 12)
         signals(0, 0, W, "x")
-        exposures(1, 0, P, nc.vector)
-        for j0, j1 in ((128, 192), (192, 256), (256, 512)):
+        for j0, j1 in ((0, 32), (32, 256), (256, 512)):
             exposures(1, j0, j1, nc.gpsimd)
-        damp_loadings(3, [(0, 256, 5)])
+        both = slot_tile(5, [P, 2, 4, 256], F32, "damped3")
+        damped[3, 0] = both[:, 0]
+        damped[3, 256] = both[:, 1]
+        damp_loadings(3, [(0, 256, None)])
         late = slot_tile(13, [P, 2, 4, 256], F32, "carry_late")
         carry[1, W] = late[:, 0]
         carry[1, W + 256] = late[:, 1]
@@ -328,7 +331,7 @@ def tile_list_regime_damped_signals_kernel(
         signals(1, 0, W, "x")
         store(0, W, False)
         exposures(1, W, W + 256, nc.gpsimd)
-        damp_loadings(3, [(256, W, 16)])
+        damp_loadings(3, [(256, W, None)])
         signals(0, W, W + 256, "z")
         signals(0, W + 256, S, "x")
         for t in range(1, 4):
@@ -336,7 +339,10 @@ def tile_list_regime_damped_signals_kernel(
         quantise_h(1, W, W + 256, 3)
         signals(1, W, W + 256, "z")
         store(W, W + 256, False)
-        exposures(1, W + 256, S, nc.vector)
+        planes = slot_tile(17, [P, 4, 256], BF16, "h_planes")
+        nc.vector.tensor_tensor(planes[:], damped[3, 256], carry[1, W + 256], ALU.add)
+        nc.vector.tensor_copy(h_at(1, W + 256, S).rearrange("p (c i t) -> p c t i", i=4, t=4),
+                              planes[:].rearrange("p t (c i) -> p c t i", i=4))
         quantise_h(1, W + 256, S, 9)
         signals(1, W + 256, S, "x")
         store(W + 256, S, True)

@@ -210,12 +210,9 @@ def tile_list_regime_damped_signals_kernel(
                     if (A, base) == (0, 0):
                         h_bf16[A, base] = keep.tile([P, 4 * W], BF16, name="h_first", align_bytes=64)
                     else:
-                        pair = slot_tile(20, [P, 2, 4 * W], BF16, "h_pair")
-                        h_bf16[0, W] = pair[:, 0, :]
-                        h_bf16[1, 0] = pair[:, 1, :]
-                        h_bf16["pair"] = pair
+                        h_bf16[A, base] = slot_tile(20 if A else 22, [P, 4 * W], BF16, "h_half%d" % A)
                 else:
-                    h_bf16[A, base] = slot_tile(20 if base == W else 21, [P, 4 * width], BF16, "h_last%d" % base)
+                    h_bf16[A, base] = slot_tile(20, [P, 4 * width], BF16, "h_last%d" % base)
             return h_bf16[A, base][:, 4 * (j0 - base):4 * (j1 - base)]
 
         def exposures(A, j0, j1, eng):
@@ -242,9 +239,8 @@ def tile_list_regime_damped_signals_kernel(
             codes = slot_tile(slot, [P, 2, W], U32, "h_codes_pair")
             h_codes[0, W] = codes[:, 0, :]
             h_codes[1, 0] = codes[:, 1, :]
-            nc.vector.quantize_mx(
-                codes[:].rearrange("p u j -> p (u j)").bitcast(FP8X4), h_sc[:, 1:3, :].rearrange("p u j -> p (u j)"),
-                h_bf16["pair"][:].rearrange("p u j -> p (u j)"))
+            nc.vector.quantize_mx(codes[:, 0, :].bitcast(FP8X4), h_sc[:, 1, :], h_bf16[0, W][:])
+            nc.vector.quantize_mx(codes[:, 1, :].bitcast(FP8X4), h_sc[:, 2, :], h_bf16[1, 0][:])
 
         y_ps = {}
 
@@ -298,7 +294,7 @@ def tile_list_regime_damped_signals_kernel(
         for j0, j1 in ((0, 256), (256, 384), (384, 512)):
             exposures(0, j0, j1, nc.gpsimd)
         damp_loadings(1, [(0, W, 8)])
-        for j0, j1 in ((512, 640), (640, 768), (768, 1024)):
+        for j0, j1 in ((512, 640), (640, 768), (768, 896), (896, 1024)):
             exposures(0, j0, j1, nc.gpsimd)
         cast_wa(1, 1, False)
         damping(3, [(0, 256, 13), (256, W, 15)])
@@ -307,19 +303,16 @@ def tile_list_regime_damped_signals_kernel(
         loadings(2)
         damp_loadings(2, [(0, 32, 5), (32, W, 7)])
         loadings(3)
-        for q in range(2):
-            carry[1, 256 * q] = slot_tile(16 + q, [P, 4, 256], F32, "carry1_%d" % q)
-        for t in range(4):
-            for j0 in range(0, W, 256):
-                gather_carry(1, t, j0, j0 + 256)
+        carry[1, 0] = slot_tile(16, [P, 4, W], F32, "carry1")[:]
+        for t in range(3):
+            gather_carry(1, t, 0, W)
+        for j0 in range(0, W, 256):
+            gather_carry(1, 3, j0, j0 + 256)
         quantise_h(0, 0, W, 12)
         signals(0, 0, W, "x")
         for j0, j1 in ((0, 32), (32, 256), (256, 512)):
             exposures(1, j0, j1, nc.gpsimd)
-        both = slot_tile(5, [P, 2, 4, 256], F32, "damped3")
-        damped[3, 0] = both[:, 0]
-        damped[3, 256] = both[:, 1]
-        damp_loadings(3, [(0, 256, None)])
+        damp_loadings(3, [(0, 256, 5)])
         late = slot_tile(13, [P, 2, 4, 256], F32, "carry_late")
         carry[1, W] = late[:, 0]
         carry[1, W + 256] = late[:, 1]
@@ -331,7 +324,7 @@ def tile_list_regime_damped_signals_kernel(
         signals(1, 0, W, "x")
         store(0, W, False)
         exposures(1, W, W + 256, nc.gpsimd)
-        damp_loadings(3, [(256, W, None)])
+        damp_loadings(3, [(256, W, 22)])
         signals(0, W, W + 256, "z")
         signals(0, W + 256, S, "x")
         for t in range(1, 4):
@@ -339,10 +332,7 @@ def tile_list_regime_damped_signals_kernel(
         quantise_h(1, W, W + 256, 3)
         signals(1, W, W + 256, "z")
         store(W, W + 256, False)
-        planes = slot_tile(17, [P, 4, 256], BF16, "h_planes")
-        nc.vector.tensor_tensor(planes[:], damped[3, 256], carry[1, W + 256], ALU.add)
-        nc.vector.tensor_copy(h_at(1, W + 256, S).rearrange("p (c i t) -> p c t i", i=4, t=4),
-                              planes[:].rearrange("p t (c i) -> p c t i", i=4))
+        exposures(1, W + 256, S, nc.vector)
         quantise_h(1, W + 256, S, 9)
         signals(1, W + 256, S, "x")
         store(W + 256, S, True)

@@ -312,27 +312,35 @@ def tile_list_regime_damped_signals_kernel(
         signals(0, 0, W, "x")
         for j0, j1 in ((0, 32), (32, 256), (256, 512)):
             exposures(1, j0, j1, nc.gpsimd)
-        damp_loadings(3, [(0, 256, 5)])
-        late = slot_tile(13, [P, 2, 4, 256], F32, "carry_late")
-        carry[1, W] = late[:, 0]
-        carry[1, W + 256] = late[:, 1]
-        gather_carry(1, 0, W, W + 256)
-        gather_carry(1, 0, W + 256, S)
-        for t in range(1, 4):
+        both = slot_tile(5, [P, 2, 4, 256], F32, "damped3")
+        damped[3, 0] = both[:, 0]
+        damped[3, 256] = both[:, 1]
+        damp_loadings(3, [(0, 256, None)])
+        carry[1, W] = slot_tile(13, [P, 4, 256], F32, "carry_third")[:]
+        for t in range(4):
             gather_carry(1, t, W, W + 256)
-        quantise_pair(0)
+        damp_loadings(3, [(256, W, None)])
+        quantise_pair(7)
         signals(1, 0, W, "x")
         store(0, W, False)
         exposures(1, W, W + 256, nc.gpsimd)
-        damp_loadings(3, [(256, W, 22)])
+        carry[1, W + 256] = slot_tile(22, [P, 4, 256], F32, "carry_last")[:]
         signals(0, W, W + 256, "z")
         signals(0, W + 256, S, "x")
-        for t in range(1, 4):
+        for t in range(4):
             gather_carry(1, t, W + 256, S)
         quantise_h(1, W, W + 256, 3)
         signals(1, W, W + 256, "z")
         store(W, W + 256, False)
-        exposures(1, W + 256, S, nc.vector)
-        quantise_h(1, W + 256, S, 9)
-        signals(1, W + 256, S, "x")
+        for j0 in (W + 256, W + 384):
+            exposures(1, j0, j0 + P, nc.vector)
+        for j0 in (W + 256, W + 384):
+            quantise_h(1, j0, j0 + P, 9 if j0 == W + 256 else 11)
+        for j0 in (W + 256, W + 384):
+            for c in range(4):
+                nc.tensor.matmul_mx(
+                    y_ps[W + 256, c][:, j0 - W - 256:j0 - W - 128], lhsT=wf_codes[:, 1, P * c:P * (c + 1)].bitcast(FP8X4),
+                    lhsT_scale=wf_sc[:].bitcast(U8)[4:P, P * c:P * (c + 1)],
+                    rhs=h_codes[1, j0].bitcast(FP8X4), rhs_scale=h_sc[:, 3, j0 - W:j0 - W + P],
+                    start=False, stop=(j0 == W + 384))
         store(W + 256, S, True)

@@ -18,6 +18,9 @@ ALU = mybir.AluOpType
 
 P = 128
 W = 512
+Q = 256
+E = 128
+LEAD = 32
 
 
 def tile_list_regime_damped_signals_kernel(
@@ -27,7 +30,7 @@ def tile_list_regime_damped_signals_kernel(
     nc = tc.nc
     with ExitStack() as ctx:
         keep = ctx.enter_context(tc.tile_pool(name="keep", bufs=1))
-        slots = ctx.enter_context(tc.tile_pool(name="slots", bufs=1))
+        shared = ctx.enter_context(tc.tile_pool(name="shared", bufs=1))
         work = ctx.enter_context(tc.tile_pool(name="work", bufs=2))
         psum = ctx.enter_context(tc.psum_pool(name="psum", bufs=4))
 
@@ -42,226 +45,199 @@ def tile_list_regime_damped_signals_kernel(
         wb_sc = keep.tile([P, H], U8, name="wb_sc", align_bytes=64)
         bias_t = keep.tile([P, 4], F32, name="bias_t")
         one = keep.tile([P, 1], F32, name="one")
-        warm = keep.tile([P, 1], F32, name="warm")
         v_codes = keep.tile([P, 2, S], U32, name="v_codes", align_bytes=64)
         v_sc = keep.tile([P, S], U8, name="v_sc", align_bytes=64)
         v2_codes = keep.tile([P, S], U32, name="v2_codes", align_bytes=64)
         v2_sc = keep.tile([P, S], U8, name="v2_sc", align_bytes=64)
-        wa_codes = {}
         wa_sc = keep.tile([P, 4, W], U8, name="wa_sc", align_bytes=64)
         h_sc = keep.tile([P, 4, W], U8, name="h_sc", align_bytes=64)
 
-        def slot_tile(slot, shape, dtype, name):
-            return slots.tile(shape, dtype, name=name, tag="slot%d" % slot, align_bytes=64)
+        def buffer(tag, shape, dtype, name):
+            return shared.tile(shape, dtype, name=name, tag=tag, align_bytes=64)
+
+        def half_cols(half):
+            return slice(half * W, (half + 1) * W)
+
+        def entries(lst, j0, j1):
+            return lst[:, j0 // 16:j1 // 16]
+
+        def piece(tiles, key, c0, c1):
+            first = max(c for (k, c) in tiles if k == key and c <= c0)
+            return tiles[key, first][:, :, c0 - first:c1 - first]
 
         nc.vector.memset(v_sc_win[:], 0)
         nc.gpsimd.memset(wb_sc_raw[:], 0)
         nc.gpsimd.memset(one[:], 1.0)
         nc.gpsimd.memset(wf_sc[:], 0)
 
-        def load_words(slot, words, name):
-            win = slot_tile(slot, [P, T], I32, name)
-            nc.sync.dma_start(win[:], words.rearrange("p t i -> p (t i)").bitcast(I32))
+        wa_raw, g_win, v_win = {}, {}, {}
+        gT_lanes = gT.rearrange("(blk p t) j -> blk t p j", blk=2, t=4)
+        wa_rows = wa.rearrange("(kp p i) r -> kp p i r", kp=2, i=4)
+
+        def load_words(tag, words, name):
+            win = buffer(tag, [P, T], I32, name)
+            nc.sync.dma_start(win[:], words.rearrange("p j i -> p (j i)").bitcast(I32))
             return win
 
-        wa_raw = {}
-        g_win = {}
-        v_win = {}
-        gT_v = gT.rearrange("(A p i) t -> A i p t", A=2, i=4)
-        wa_v = wa.rearrange("(a p j) r -> a p j r", a=2, j=4)
+        def load_wa(tag, blk, kp):
+            wa_raw[blk, kp] = buffer(tag, [P, 4, W], F32, "wa_raw%d%d" % (blk, kp))
+            nc.sync.dma_start(wa_raw[blk, kp][:], wa_rows[kp, :, :, blk * W:(blk + 1) * W])
 
-        def load_wa(slot, A, a):
-            wa_raw[A, a] = slot_tile(slot, [P, 4, W], F32, "wa_raw%d%d" % (A, a))
-            nc.sync.dma_start(wa_raw[A, a][:], wa_v[a, :, :, A * W:(A + 1) * W])
+        def load_g(tag, blk, t):
+            g_win[blk, t] = buffer(tag, [P, T], F32, "g_win%d%d" % (blk, t))
+            nc.sync.dma_start(g_win[blk, t][:], gT_lanes[blk, t])
 
-        def load_g(slot, A, t):
-            g_win[A, t] = slot_tile(slot, [P, T], F32, "g_win%d%d" % (A, t))
-            nc.sync.dma_start(g_win[A, t][:], gT_v[A, t])
-
-        def load_plane(a):
+        def load_v_plane(kp):
             for q in range(4):
-                p0 = 32 * q + 4 * (a + 1)
-                nc.sync.dma_start(v_sc_win[p0:p0 + 4, :], tab_scales[a, 4 * q:4 * q + 4, :].bitcast(I32))
+                p0 = 32 * q + 4 * (kp + 1)
+                nc.sync.dma_start(v_sc_win[p0:p0 + 4, :], tab_scales[kp, 4 * q:4 * q + 4, :].bitcast(I32))
 
         nc.sync.dma_start(idx2[:], offs2)
         for q in range(4):
             four = tab2_scales[0, 4 * q:4 * q + 4, :].bitcast(I32)
             nc.sync.dma_start(v2_sc_win[32 * q:32 * q + 32, :], four.unsqueeze(0).broadcast_to([8, 4, T // 4]))
         nc.sync.dma_start(wb_raw[:], wb_words[0].bitcast(I32))
-        v2_win = load_words(0, tab2_words[0], "v2_win")
+        v2_win = load_words("v2_win", tab2_words[0], "v2_win")
         nc.sync.dma_start(idx[:], offs)
         for q in range(4):
             nc.sync.dma_start(wb_sc_raw[32 * q:32 * q + 4, :], wb_scales[0, 4 * q:4 * q + 4, :].bitcast(I32))
-        v_win[0] = load_words(1, tab_words[0], "v_win0")
-        load_plane(0)
-        nc.scalar.activation(warm[:], one[:], ACT.Abs_reciprocal_sqrt, bias=one[:])
-        load_wa(5, 0, 0)
-        load_plane(1)
-        v_win[1] = load_words(2, tab_words[1], "v_win1")
-        load_g(3, 0, 0)
-        load_wa(7, 0, 1)
-        load_g(4, 0, 1)
-        load_g(6, 0, 2)
-        load_wa(9, 1, 0)
-        load_g(8, 0, 3)
-        load_wa(13, 1, 1)
-        load_g(0, 1, 0)
-        load_g(1, 1, 1)
-        load_g(14, 1, 2)
-        load_g(3, 1, 3)
+        v_win[0] = load_words("v_win0", tab_words[0], "v_win0")
+        load_v_plane(0)
+        load_wa("wa_raw00", 0, 0)
+        load_v_plane(1)
+        v_win[1] = load_words("v_win1", tab_words[1], "v_win1")
+        load_g("g_win00", 0, 0)
+        load_wa("wa_raw01", 0, 1)
+        load_g("g_win01", 0, 1)
+        load_g("g_win02", 0, 2)
+        load_wa("wa_raw10", 1, 0)
+        load_g("g_win03", 0, 3)
+        load_wa("wa_raw11", 1, 1)
+        load_g("v2_win", 1, 0)
+        load_g("v_win0", 1, 1)
+        load_g("g_win12", 1, 2)
+        load_g("g_win00", 1, 3)
         for q in range(4):
             nc.sync.dma_start(wf_sc[32 * q:32 * q + 8, :], wf_scales[:, 4 * q:4 * q + 4, :].bitcast(I32))
         with nc.allow_non_contiguous_dma(reason="one bias value a partition"):
             nc.sync.dma_start(bias_t[:], bias.rearrange("(c p) -> p c", p=P))
 
-        def cols(half):
-            return slice(half * W, (half + 1) * W)
-
-        def part(lst, j0, j1):
-            return lst[:, j0 // 16:j1 // 16]
-
-        def permute_wb(A):
+        def reorder_wb(blk):
             nc.vector.tensor_copy(
-                wb_codes[:].bitcast(U16)[:, cols(A)].rearrange("p (t m) -> p t m", t=4),
-                wb_raw[:].bitcast(U16)[:, cols(A)].rearrange("p (m t) -> p t m", t=4))
+                wb_codes[:].bitcast(U16)[:, half_cols(blk)].rearrange("p (t m) -> p t m", t=4),
+                wb_raw[:].bitcast(U16)[:, half_cols(blk)].rearrange("p (m t) -> p t m", t=4))
             nc.gpsimd.tensor_copy(
-                wb_sc[:, cols(A)].rearrange("p (t m) -> p t m", t=4),
-                wb_sc_raw[:].bitcast(U8)[:, cols(A)].rearrange("p (m t) -> p t m", t=4))
+                wb_sc[:, half_cols(blk)].rearrange("p (t m) -> p t m", t=4),
+                wb_sc_raw[:].bitcast(U8)[:, half_cols(blk)].rearrange("p (m t) -> p t m", t=4))
 
         damp = {}
 
-        def damping(u, parts):
-            A, half = divmod(u, 2)
-            for i0, i1, slot in parts:
-                damp[u, i0] = slot_tile(slot, [P, 4, i1 - i0], F32, "damp%d_%d" % (u, i0))
+        def damping(u, ring, parts):
+            blk, half = divmod(u, 2)
+            for i0, i1, tag in parts:
+                damp[u, i0] = buffer(tag, [P, 4, i1 - i0], F32, "damp%d_%d" % (u, i0))
             for t in range(4):
-                c = 4 * A + t
-                b_ps = psum.tile([P, W], F32, name="b_ps", tag=("z" if u == 3 else "x"))
+                c = 4 * blk + t
+                b_ps = psum.tile([P, W], F32, name="b_ps", tag=ring)
                 nc.tensor.matmul_mx(
-                    b_ps[:], lhsT=wb_codes[:, 256 * c:256 * (c + 1)].bitcast(FP4X4), lhsT_scale=wb_sc[:, P * c:P * (c + 1)],
-                    rhs=v2_codes[:, cols(half)].bitcast(FP8X4), rhs_scale=v2_sc[:, cols(half)], start=True, stop=True)
-                for i0, i1, slot in parts:
+                    b_ps[:], lhsT=wb_codes[:, 2 * P * c:2 * P * (c + 1)].bitcast(FP4X4),
+                    lhsT_scale=wb_sc[:, P * c:P * (c + 1)],
+                    rhs=v2_codes[:, half_cols(half)].bitcast(FP8X4), rhs_scale=v2_sc[:, half_cols(half)],
+                    start=True, stop=True)
+                for i0, i1, tag in parts:
                     nc.scalar.activation(damp[u, i0][:, t, :], b_ps[:, i0:i1], ACT.Abs)
-            step = 2 * len(parts)
-            runs = [damp[u, i0][:, t:t + step, :] for i0, i1, slot in parts for t in range(0, 4, step)]
-            for d in runs:
-                nc.scalar.activation(d, d, ACT.Abs_reciprocal_sqrt, bias=one[:])
-            for d in runs:
-                nc.scalar.activation(d, d, ACT.Square)
+            lanes = 2 * len(parts)
+            runs = [damp[u, i0][:, t:t + lanes, :] for i0, i1, tag in parts for t in range(0, 4, lanes)]
+            for run in runs:
+                nc.scalar.activation(run, run, ACT.Abs_reciprocal_sqrt, bias=one[:])
+            for run in runs:
+                nc.scalar.activation(run, run, ACT.Square)
 
-        grouped = {}
+        wa_bf16, wa_codes = {}, {}
 
-        def cast_wa(A, a, on_pool):
-            if True:
-                grouped[A, a] = work.tile([P, 4 * W], BF16, name="wa_grouped", align_bytes=64)
-                dst = grouped[A, a][:].rearrange("p (t m j) -> p m t j", t=4, j=4)
-                src = wa_raw[A, a][:].rearrange("p j (m t) -> p m t j", t=4)
-                if on_pool:
-                    nc.gpsimd.tensor_scalar(dst, src, 1.0, 0.0, ALU.mult, ALU.add)
-                else:
-                    nc.scalar.copy(dst, src)
+        def round_wa(blk, kp, eng):
+            wa_bf16[blk, kp] = work.tile([P, 4 * W], BF16, name="wa_bf16", align_bytes=64)
+            dst = wa_bf16[blk, kp][:].rearrange("p (t m i) -> p m t i", t=4, i=4)
+            src = wa_raw[blk, kp][:].rearrange("p i (m t) -> p m t i", t=4)
+            if eng == "gpsimd":
+                nc.gpsimd.tensor_scalar(dst, src, 1.0, 0.0, ALU.mult, ALU.add)
+            else:
+                nc.scalar.copy(dst, src)
 
-        def quantise_wa(A, a):
-            if True:
-                wa_codes[A, a] = slot_tile({(0, 0): 2, (0, 1): 4, (1, 0): 31, (1, 1): 32}[A, a], [P, W], U32, "wa_codes%d%d" % (A, a))
-                nc.vector.quantize_mx(wa_codes[A, a][:].bitcast(FP8X4), wa_sc[:, 2 * A + a, :], grouped[A, a][:])
+        def quantise_wa(blk, kp, tag):
+            wa_codes[blk, kp] = buffer(tag, [P, W], U32, "wa_codes%d%d" % (blk, kp))
+            nc.vector.quantize_mx(wa_codes[blk, kp][:].bitcast(FP8X4), wa_sc[:, 2 * blk + kp, :], wa_bf16[blk, kp][:])
 
         carry = {}
 
-        def carry_at(A, j0, j1):
-            base = max(b for (a, b) in carry if a == A and b <= j0)
-            return carry[A, base][:, :, j0 - base:j1 - base]
-
-        def gather_carry(A, t, j0, j1):
-            nc.vector.tensor_copy(carry_at(A, j0, j1)[:, t, :], g_win[A, t][:].indirect(part(idx, j0, j1)))
+        def gather_carry(blk, t, j0, j1):
+            nc.vector.tensor_copy(piece(carry, blk, j0, j1)[:, t, :], g_win[blk, t][:].indirect(entries(idx, j0, j1)))
 
         a_ps = {}
 
-        def loadings(u):
-            A, half = divmod(u, 2)
+        def loadings(u, ring):
+            blk, half = divmod(u, 2)
+            passes = (1, 0) if half else (0, 1)
             for t in range(4):
-                a_ps[u, t] = psum.tile([P, W], F32, name="a_ps", tag=("x" if u in (1, 2) else "z"))
-                order = (1, 0) if half else (0, 1)
-                for a in order:
+                a_ps[u, t] = psum.tile([P, W], F32, name="a_ps", tag=ring)
+                for kp in passes:
                     nc.tensor.matmul_mx(
-                        a_ps[u, t][:], lhsT=wa_codes[A, a][:, P * t:P * (t + 1)].bitcast(FP8X4),
-                        lhsT_scale=wa_sc[:, 2 * A + a, P * t:P * (t + 1)],
-                        rhs=v_codes[:, a, cols(half)].bitcast(FP8X4), rhs_scale=v_sc[4 * (a + 1):P, cols(half)],
-                        start=(a == order[0]), stop=(a == order[1]))
+                        a_ps[u, t][:], lhsT=wa_codes[blk, kp][:, P * t:P * (t + 1)].bitcast(FP8X4),
+                        lhsT_scale=wa_sc[:, 2 * blk + kp, P * t:P * (t + 1)],
+                        rhs=v_codes[:, kp, half_cols(half)].bitcast(FP8X4),
+                        rhs_scale=v_sc[4 * (kp + 1):P, half_cols(half)],
+                        start=(kp == passes[0]), stop=(kp == passes[1]))
 
         damped = {}
 
-        def damp_loadings(u, parts):
-            for i0, i1, slot in parts:
-                if slot is not None:
-                    damped[u, i0] = slot_tile(slot, [P, 4, i1 - i0], F32, "damped%d_%d" % (u, i0))[:]
+        def damp_loadings(u, ranges):
             for t in range(4):
-                for i0, i1, slot in parts:
-                    base = max(b for (v, b) in damp if v == u and b <= i0)
-                    nc.vector.tensor_tensor(damped[u, i0][:, t, :], a_ps[u, t][:, i0:i1], damp[u, base][:, t, i0 - base:i1 - base], ALU.mult)
+                for i0, i1 in ranges:
+                    nc.vector.tensor_tensor(
+                        damped[u, i0][:, t, :], a_ps[u, t][:, i0:i1], piece(damp, u, i0, i1)[:, t, :], ALU.mult)
 
         h_bf16 = {}
 
-        def h_at(A, j0, j1):
-            width = 256 if (A == 1 and j0 >= W) else W
-            base = j0 // width * width
-            if (A, base) not in h_bf16:
-                if width == W:
-                    if (A, base) == (0, 0):
-                        h_bf16[A, base] = keep.tile([P, 4 * W], BF16, name="h_first", align_bytes=64)
-                    else:
-                        h_bf16[A, base] = slot_tile(20 if A else 22, [P, 4 * W], BF16, "h_half%d" % A)
-                else:
-                    h_bf16[A, base] = slot_tile(20, [P, 4 * width], BF16, "h_last%d" % base)
-            return h_bf16[A, base][:, 4 * (j0 - base):4 * (j1 - base)]
+        def h_cols(blk, j0, j1):
+            first = max(j for (b, j) in h_bf16 if b == blk and j <= j0)
+            return h_bf16[blk, first][:, 4 * (j0 - first):4 * (j1 - first)]
 
-        def exposures(A, j0, j1, eng):
+        def exposures(eng, blk, j0, j1):
             half, i0 = divmod(j0, W)
-            u = 2 * A + half
-            i1 = i0 + j1 - j0
-            dst = h_at(A, j0, j1).rearrange("p (c i t) -> p c t i", i=4, t=4)
-            base = max(b for (v, b) in damped if v == u and b <= i0)
-            q = damped[u, base][:, :, i0 - base:i1 - base].rearrange("p t (c i) -> p c t i", i=4)
-            g = carry_at(A, j0, j1).rearrange("p t (c i) -> p c t i", i=4)
-            eng.tensor_tensor(dst, q, g, ALU.add)
+            eng.tensor_tensor(
+                h_cols(blk, j0, j1).rearrange("p (c i t) -> p c t i", i=4, t=4),
+                piece(damped, 2 * blk + half, i0, i0 + j1 - j0).rearrange("p t (c i) -> p c t i", i=4),
+                piece(carry, blk, j0, j1).rearrange("p t (c i) -> p c t i", i=4), ALU.add)
 
         h_codes = {}
 
-        def quantise_h(A, j0, j1, slot):
+        def quantise_h(blk, j0, j1):
             half, i0 = divmod(j0, W)
-            u = 2 * A + half
-            i1 = i0 + j1 - j0
-            if True:
-                h_codes[A, j0] = slot_tile(slot, [P, j1 - j0], U32, "h_codes%d_%d" % (A, j0))[:]
-            nc.vector.quantize_mx(h_codes[A, j0].bitcast(FP8X4), h_sc[:, u, i0:i1], h_at(A, j0, j1))
-
-        def quantise_pair(slot):
-            codes = slot_tile(slot, [P, 2, W], U32, "h_codes_pair")
-            h_codes[0, W] = codes[:, 0, :]
-            h_codes[1, 0] = codes[:, 1, :]
-            nc.vector.quantize_mx(codes[:, 0, :].bitcast(FP8X4), h_sc[:, 1, :], h_bf16[0, W][:])
-            nc.vector.quantize_mx(codes[:, 1, :].bitcast(FP8X4), h_sc[:, 2, :], h_bf16[1, 0][:])
+            nc.vector.quantize_mx(
+                h_codes[blk, j0].bitcast(FP8X4), h_sc[:, 2 * blk + half, i0:i0 + j1 - j0], h_cols(blk, j0, j1))
 
         y_ps = {}
 
-        def signals(A, j0, j1, tag):
+        def signals(blk, j0, j1, y0, stop):
             half, i0 = divmod(j0, W)
-            u = 2 * A + half
-            i1 = i0 + j1 - j0
-            base = max(b for (a, b) in h_codes if a == A and b <= j0)
+            first = max(j for (b, j) in h_codes if b == blk and j <= j0)
             for c in range(4):
-                if A == 0:
-                    y_ps[j0, c] = psum.tile([P, j1 - j0], F32, name="y_ps", tag=tag)
                 nc.tensor.matmul_mx(
-                    y_ps[j0, c][:], lhsT=wf_codes[:, A, P * c:P * (c + 1)].bitcast(FP8X4),
-                    lhsT_scale=wf_sc[:].bitcast(U8)[4 * A:P, P * c:P * (c + 1)],
-                    rhs=h_codes[A, base][:, j0 - base:j1 - base].bitcast(FP8X4), rhs_scale=h_sc[:, u, i0:i1],
-                    start=(A == 0), stop=(A == 1))
+                    y_ps[y0, c][:, j0 - y0:j1 - y0], lhsT=wf_codes[:, blk, P * c:P * (c + 1)].bitcast(FP8X4),
+                    lhsT_scale=wf_sc[:].bitcast(U8)[4 * blk:P, P * c:P * (c + 1)],
+                    rhs=h_codes[blk, first][:, j0 - first:j1 - first].bitcast(FP8X4),
+                    rhs_scale=h_sc[:, 2 * blk + half, i0:i0 + j1 - j0],
+                    start=(blk == 0), stop=stop)
 
-        def store(j0, j1, share):
+        def open_signals(j0, j1, ring):
+            for c in range(4):
+                y_ps[j0, c] = psum.tile([P, j1 - j0], F32, name="y_ps", tag=ring)
+            signals(0, j0, j1, j0, False)
+
+        def store(j0, j1, with_vector):
             for c in range(4):
                 y = work.tile([P, j1 - j0], F32, name="y", bufs=8)
-                if share and c % 2 == 1:
+                if with_vector and c % 2 == 1:
                     nc.vector.tensor_scalar(y[:], y_ps[j0, c][:], bias_t[:, c:c + 1], None, ALU.add)
                 else:
                     nc.scalar.activation(y[:], y_ps[j0, c][:], ACT.Identity, bias=bias_t[:, c:c + 1])
@@ -269,78 +245,97 @@ def tile_list_regime_damped_signals_kernel(
 
         nc.vector.tensor_copy(v2_sc[:], v2_sc_win[:].bitcast(U8).indirect(idx2[:]))
         for half in range(2):
-            permute_wb(half)
-            nc.vector.tensor_copy(v2_codes[:, cols(half)], v2_win[:].bitcast(U32).indirect(part(idx2, half * W, (half + 1) * W)))
-        damping(0, [(0, W, 10)])
-        damping(1, [(0, W, 11)])
-        damping(2, [(0, 32, 12), (32, W, 15)])
+            reorder_wb(half)
+            nc.vector.tensor_copy(
+                v2_codes[:, half_cols(half)], v2_win[:].bitcast(U32).indirect(entries(idx2, half * W, (half + 1) * W)))
+        damping(0, "x", [(0, W, "damp0")])
+        damping(1, "x", [(0, W, "damp1")])
+        damping(2, "x", [(0, LEAD, "damp2_lead"), (LEAD, W, "damp2_rest")])
         nc.vector.tensor_copy(v_sc[:], v_sc_win[:].bitcast(U8).indirect(idx[:]))
-        for a in range(2):
-            nc.vector.tensor_copy(v_codes[:, a, :], v_win[a][:].bitcast(U32).indirect(idx[:]))
-        for a in range(2):
-            cast_wa(0, a, True)
-            quantise_wa(0, a)
-        wf_codes = slot_tile(4, [P, 2, N], I32, "wf_codes")
-        nc.sync.dma_start(wf_codes[:], wf_words.rearrange("a p e i -> p a (e i)").bitcast(I32))
+        for kp in range(2):
+            nc.vector.tensor_copy(v_codes[:, kp, :], v_win[kp][:].bitcast(U32).indirect(idx[:]))
+
+        round_wa(0, 0, "gpsimd")
+        quantise_wa(0, 0, "v_win1")
+        round_wa(0, 1, "gpsimd")
+        quantise_wa(0, 1, "g_win01")
+        wf_codes = buffer("g_win01", [P, 2, N], I32, "wf_codes")
+        nc.sync.dma_start(wf_codes[:], wf_words.rearrange("blk p n i -> p blk (n i)").bitcast(I32))
         carry[0, 0] = keep.tile([P, 4, S], F32, name="carry0")
         for t in range(3):
             gather_carry(0, t, 0, S)
-        loadings(0)
-        damp_loadings(0, [(0, W, 6)])
+        loadings(0, "z")
+        damped[0, 0] = buffer("g_win02", [P, 4, W], F32, "damped0")
+        damp_loadings(0, [(0, W)])
         gather_carry(0, 3, 0, W)
         gather_carry(0, 3, W, S)
-        loadings(1)
-        cast_wa(1, 0, True)
-        for j0, j1 in ((0, 256), (256, 384), (384, 512)):
-            exposures(0, j0, j1, nc.gpsimd)
-        damp_loadings(1, [(0, W, 8)])
-        for j0, j1 in ((512, 640), (640, 768), (768, 896), (896, 1024)):
-            exposures(0, j0, j1, nc.gpsimd)
-        cast_wa(1, 1, False)
-        damping(3, [(0, 256, 13), (256, W, 15)])
-        quantise_wa(1, 0)
-        quantise_wa(1, 1)
-        loadings(2)
-        damp_loadings(2, [(0, 32, 5), (32, W, 7)])
-        loadings(3)
-        carry[1, 0] = slot_tile(16, [P, 4, W], F32, "carry1")[:]
+        loadings(1, "x")
+        round_wa(1, 0, "gpsimd")
+        h_bf16[0, 0] = keep.tile([P, 4 * W], BF16, name="h_bf16_00", align_bytes=64)
+        exposures(nc.gpsimd, 0, 0, Q)
+        for j0 in range(Q, W, E):
+            exposures(nc.gpsimd, 0, j0, j0 + E)
+        damped[1, 0] = buffer("g_win03", [P, 4, W], F32, "damped1")
+        damp_loadings(1, [(0, W)])
+        h_bf16[0, W] = buffer("h_bf16_01", [P, 4 * W], BF16, "h_bf16_01")
+        for j0 in range(W, S, E):
+            exposures(nc.gpsimd, 0, j0, j0 + E)
+
+        round_wa(1, 1, "scalar")
+        damping(3, "z", [(0, Q, "wa_raw11"), (Q, W, "damp2_rest")])
+        quantise_wa(1, 0, "wa_codes10")
+        quantise_wa(1, 1, "wa_codes11")
+        loadings(2, "x")
+        damped[2, 0] = buffer("wa_raw00", [P, 4, LEAD], F32, "damped2_lead")
+        damped[2, LEAD] = buffer("wa_raw01", [P, 4, W - LEAD], F32, "damped2_rest")
+        damp_loadings(2, [(0, LEAD), (LEAD, W)])
+        loadings(3, "z")
+        carry[1, 0] = buffer("carry1", [P, 4, W], F32, "carry1")
         for t in range(3):
             gather_carry(1, t, 0, W)
-        for j0 in range(0, W, 256):
-            gather_carry(1, 3, j0, j0 + 256)
-        quantise_h(0, 0, W, 12)
-        signals(0, 0, W, "x")
-        for j0, j1 in ((0, 32), (32, 256), (256, 512)):
-            exposures(1, j0, j1, nc.gpsimd)
-        both = slot_tile(5, [P, 2, 4, 256], F32, "damped3")
-        damped[3, 0] = both[:, 0]
-        damped[3, 256] = both[:, 1]
-        damp_loadings(3, [(0, 256, None)])
-        carry[1, W] = slot_tile(13, [P, 4, 256], F32, "carry_third")[:]
+        for j0 in range(0, W, Q):
+            gather_carry(1, 3, j0, j0 + Q)
+        h_codes[0, 0] = buffer("damp2_lead", [P, W], U32, "h_codes00")[:]
+        quantise_h(0, 0, W)
+        open_signals(0, W, "x")
+        h_bf16[1, 0] = buffer("h_bf16_10", [P, 4 * W], BF16, "h_bf16_10")
+        for j0, j1 in ((0, LEAD), (LEAD, Q), (Q, W)):
+            exposures(nc.gpsimd, 1, j0, j1)
+
+        damped3 = buffer("wa_raw00", [P, 2, 4, Q], F32, "damped3")
+        damped[3, 0] = damped3[:, 0]
+        damped[3, Q] = damped3[:, 1]
+        damp_loadings(3, [(0, Q)])
+        carry[1, W] = buffer("wa_raw11", [P, 4, Q], F32, "carry1_third")
         for t in range(4):
-            gather_carry(1, t, W, W + 256)
-        damp_loadings(3, [(256, W, None)])
-        quantise_pair(7)
-        signals(1, 0, W, "x")
+            gather_carry(1, t, W, W + Q)
+        damp_loadings(3, [(Q, W)])
+        pair = buffer("wa_raw01", [P, 2, W], U32, "h_codes_pair")
+        h_codes[0, W] = pair[:, 0, :]
+        h_codes[1, 0] = pair[:, 1, :]
+        quantise_h(0, W, S)
+        quantise_h(1, 0, W)
+        signals(1, 0, W, 0, True)
         store(0, W, False)
-        exposures(1, W, W + 256, nc.gpsimd)
-        carry[1, W + 256] = slot_tile(22, [P, 4, 256], F32, "carry_last")[:]
-        signals(0, W, W + 256, "z")
-        signals(0, W + 256, S, "x")
+        h_bf16[1, W] = buffer("h_bf16_10", [P, 4 * Q], BF16, "h_bf16_third")
+        exposures(nc.gpsimd, 1, W, W + Q)
+        last = W + Q
+        carry[1, last] = buffer("h_bf16_01", [P, 4, Q], F32, "carry1_last")
+        open_signals(W, last, "z")
+        open_signals(last, S, "x")
         for t in range(4):
-            gather_carry(1, t, W + 256, S)
-        quantise_h(1, W, W + 256, 3)
-        signals(1, W, W + 256, "z")
-        store(W, W + 256, False)
-        for j0 in (W + 256, W + 384):
-            exposures(1, j0, j0 + P, nc.vector)
-        for j0 in (W + 256, W + 384):
-            quantise_h(1, j0, j0 + P, 9 if j0 == W + 256 else 11)
-        for j0 in (W + 256, W + 384):
-            for c in range(4):
-                nc.tensor.matmul_mx(
-                    y_ps[W + 256, c][:, j0 - W - 256:j0 - W - 128], lhsT=wf_codes[:, 1, P * c:P * (c + 1)].bitcast(FP8X4),
-                    lhsT_scale=wf_sc[:].bitcast(U8)[4:P, P * c:P * (c + 1)],
-                    rhs=h_codes[1, j0].bitcast(FP8X4), rhs_scale=h_sc[:, 3, j0 - W:j0 - W + P],
-                    start=False, stop=(j0 == W + 384))
-        store(W + 256, S, True)
+            gather_carry(1, t, last, S)
+        h_codes[1, W] = buffer("g_win00", [P, Q], U32, "h_codes_third")[:]
+        quantise_h(1, W, last)
+        signals(1, W, last, W, True)
+        store(W, last, False)
+
+        h_bf16[1, last] = buffer("h_bf16_10", [P, 4 * Q], BF16, "h_bf16_last")
+        for j0 in range(last, S, E):
+            exposures(nc.vector, 1, j0, j0 + E)
+        for j0, tag in ((last, "wa_raw10"), (last + E, "damp1")):
+            h_codes[1, j0] = buffer(tag, [P, E], U32, "h_codes1_%d" % j0)[:]
+            quantise_h(1, j0, j0 + E)
+        for j0 in range(last, S, E):
+            signals(1, j0, j0 + E, last, j0 + E == S)
+        store(last, S, True)

@@ -132,10 +132,8 @@ def tile_list_regime_damped_signals_kernel(
 
         damp = {}
 
-        def damping(u, ring, parts):
+        def stress(u, ring, dst):
             blk, half = divmod(u, 2)
-            for i0, i1, tag in parts:
-                damp[u, i0] = buffer(tag, [P, 4, i1 - i0], F32, "damp%d_%d" % (u, i0))
             for t in range(4):
                 c = 4 * blk + t
                 b_ps = psum.tile([P, W], F32, name="b_ps", tag=ring)
@@ -144,14 +142,13 @@ def tile_list_regime_damped_signals_kernel(
                     lhsT_scale=wb_sc[:, P * c:P * (c + 1)],
                     rhs=v2_codes[:, half_cols(half)].bitcast(FP8X4), rhs_scale=v2_sc[:, half_cols(half)],
                     start=True, stop=True)
-                for i0, i1, tag in parts:
-                    nc.scalar.activation(damp[u, i0][:, t, :], b_ps[:, i0:i1], ACT.Abs)
-            lanes = 2 * len(parts)
-            runs = [damp[u, i0][:, t:t + lanes, :] for i0, i1, tag in parts for t in range(0, 4, lanes)]
-            for run in runs:
-                nc.scalar.activation(run, run, ACT.Abs_reciprocal_sqrt, bias=one[:])
-            for run in runs:
-                nc.scalar.activation(run, run, ACT.Square)
+                nc.scalar.activation(dst[:, t, :], b_ps[:], ACT.Abs)
+
+        def take_root(run):
+            nc.scalar.activation(run, run, ACT.Abs_reciprocal_sqrt, bias=one[:])
+
+        def square(dst, src):
+            nc.scalar.activation(dst, src, ACT.Square)
 
         wa_bf16, wa_codes = {}, {}
 
@@ -248,9 +245,16 @@ def tile_list_regime_damped_signals_kernel(
             reorder_wb(half)
             nc.vector.tensor_copy(
                 v2_codes[:, half_cols(half)], v2_win[:].bitcast(U32).indirect(entries(idx2, half * W, (half + 1) * W)))
-        damping(0, "x", [(0, W, "damp0")])
-        damping(1, "x", [(0, W, "damp1")])
-        damping(2, "x", [(0, LEAD, "damp2_lead"), (LEAD, W, "damp2_rest")])
+        for u, ring in ((0, "x"), (1, "z")):
+            damp[u, 0] = buffer("damp%d" % u, [P, 4, W], F32, "damp%d" % u)
+            stress(u, ring, damp[u, 0])
+        for u in range(2):
+            take_root(damp[u, 0][:])
+        for u in range(2):
+            square(damp[u, 0][:], damp[u, 0][:])
+        root2 = buffer("root", [P, 4, W], F32, "root2")
+        stress(2, "x", root2)
+        take_root(root2[:])
         nc.vector.tensor_copy(v_sc[:], v_sc_win[:].bitcast(U8).indirect(idx[:]))
         for kp in range(2):
             nc.vector.tensor_copy(v_codes[:, kp, :], v_win[kp][:].bitcast(U32).indirect(idx[:]))
@@ -282,7 +286,15 @@ def tile_list_regime_damped_signals_kernel(
             exposures(nc.gpsimd, 0, j0, j0 + E)
 
         round_wa(1, 1, "scalar")
-        damping(3, "z", [(0, Q, "wa_raw11"), (Q, W, "damp2_rest")])
+        damp[2, 0] = buffer("wa_raw11", [P, 4, W], F32, "damp2")
+        square(damp[2, 0][:], root2[:])
+        root3 = buffer("root", [P, 4, W], F32, "root3")
+        stress(3, "z", root3)
+        for i0 in (0, Q):
+            take_root(root3[:, :, i0:i0 + Q])
+        for i0 in (0, Q):
+            damp[3, i0] = buffer("damp3_%d" % i0, [P, 4, Q], F32, "damp3_%d" % i0)
+            square(damp[3, i0][:], root3[:, :, i0:i0 + Q])
         quantise_wa(1, 0, "wa_codes10")
         quantise_wa(1, 1, "wa_codes11")
         loadings(2, "x")
@@ -295,7 +307,7 @@ def tile_list_regime_damped_signals_kernel(
             gather_carry(1, t, 0, W)
         for j0 in range(0, W, Q):
             gather_carry(1, 3, j0, j0 + Q)
-        h_codes[0, 0] = buffer("damp2_lead", [P, W], U32, "h_codes00")[:]
+        h_codes[0, 0] = buffer("wa_raw11", [P, W], U32, "h_codes00")[:]
         quantise_h(0, 0, W)
         open_signals(0, W, "x")
         h_bf16[1, 0] = buffer("h_bf16_10", [P, 4 * W], BF16, "h_bf16_10")
@@ -306,7 +318,7 @@ def tile_list_regime_damped_signals_kernel(
         damped[3, 0] = damped3[:, 0]
         damped[3, Q] = damped3[:, 1]
         damp_loadings(3, [(0, Q)])
-        carry[1, W] = buffer("wa_raw11", [P, 4, Q], F32, "carry1_third")
+        carry[1, W] = buffer("damp3_0", [P, 4, Q], F32, "carry1_third")
         for t in range(4):
             gather_carry(1, t, W, W + Q)
         damp_loadings(3, [(Q, W)])

@@ -1,6 +1,7 @@
 from contextlib import ExitStack
 
 import concourse.mybir as mybir
+from concourse.masks import make_identity
 
 K, K2, H, N, T, S = 1024, 512, 1024, 512, 2048, 1024
 FLOPS = 2 * S * (K * H + K2 * H + H * N)
@@ -45,6 +46,7 @@ def tile_list_regime_damped_signals_kernel(
         wb_sc = keep.tile([P, H], U8, name="wb_sc", align_bytes=64)
         bias_t = keep.tile([P, 4], F32, name="bias_t")
         one = keep.tile([P, 1], F32, name="one")
+        ident = keep.tile([P, P], F32, name="ident")
         v_codes = keep.tile([P, 2, S], U32, name="v_codes", align_bytes=64)
         v_sc = keep.tile([P, S], U8, name="v_sc", align_bytes=64)
         v2_codes = keep.tile([P, S], U32, name="v2_codes", align_bytes=64)
@@ -69,6 +71,7 @@ def tile_list_regime_damped_signals_kernel(
         nc.gpsimd.memset(wb_sc_raw[:], 0)
         nc.gpsimd.memset(one[:], 1.0)
         nc.gpsimd.memset(wf_sc[:], 0)
+        make_identity(nc, ident[:])
 
         wa_raw, g_win, v_win = {}, {}, {}
         gT_lanes = gT.rearrange("(blk p t) j -> blk t p j", blk=2, t=4)
@@ -152,8 +155,8 @@ def tile_list_regime_damped_signals_kernel(
 
         wa_bf16, wa_codes = {}, {}
 
-        def round_wa(blk, kp, eng):
-            wa_bf16[blk, kp] = work.tile([P, 4 * W], BF16, name="wa_bf16", align_bytes=64)
+        def round_wa(blk, kp, eng, tag):
+            wa_bf16[blk, kp] = buffer(tag, [P, 4 * W], BF16, "wa_bf16_%d%d" % (blk, kp))
             dst = wa_bf16[blk, kp][:].rearrange("p (t m i) -> p m t i", t=4, i=4)
             src = wa_raw[blk, kp][:].rearrange("p i (m t) -> p m t i", t=4)
             if eng == "gpsimd":
@@ -206,12 +209,34 @@ def tile_list_regime_damped_signals_kernel(
                 piece(damped, 2 * blk + half, i0, i0 + j1 - j0).rearrange("p t (c i) -> p c t i", i=4),
                 piece(carry, blk, j0, j1).rearrange("p t (c i) -> p c t i", i=4), ALU.add)
 
+        def exposures_on_tensor(blk, j0, ring):
+            half, i0 = divmod(j0, W)
+            rounded = []
+            for e0 in (0, E):
+                sums = psum.tile([P, 4, P], F32, name="sums", tag=ring)
+                for t in range(4):
+                    nc.tensor.matmul(sums[:, t, :], piece(damped, 2 * blk + half, i0 + e0, i0 + e0 + E)[:, t, :],
+                                     ident[:], start=True, stop=False, is_transpose=True)
+                    nc.tensor.matmul(sums[:, t, :], piece(carry, blk, j0 + e0, j0 + e0 + E)[:, t, :],
+                                     ident[:], start=False, stop=True, is_transpose=True)
+                rounded.append(buffer("rounded%d" % e0, [P, W], BF16, "rounded%d" % e0))
+                nc.scalar.copy(rounded[-1][:].rearrange("j (w c i l) -> j w c l i", w=2, i=4, l=2),
+                               sums[:].rearrange("j (w l) (c i) -> j w c l i", w=2, i=4))
+            words = psum.tile([P, 2, 2, P], F32, name="words", tag=ring)
+            for e in range(2):
+                for w in range(2):
+                    nc.tensor.transpose(words[:, e, w, :], rounded[e][:].bitcast(F32)[:, P * w:P * (w + 1)], ident[:])
+            nc.scalar.copy(
+                h_cols(blk, j0, j0 + Q).bitcast(F32).rearrange("p (e c i w) -> p e c w i", e=2, i=4, w=2),
+                words[:].rearrange("p e w (c i) -> p e c w i", i=4))
+
         h_codes = {}
 
         def quantise_h(blk, j0, j1):
             half, i0 = divmod(j0, W)
+            first = max(j for (b, j) in h_codes if b == blk and j <= j0)
             nc.vector.quantize_mx(
-                h_codes[blk, j0].bitcast(FP8X4), h_sc[:, 2 * blk + half, i0:i0 + j1 - j0], h_cols(blk, j0, j1))
+                h_codes[blk, first][:, j0 - first:j1 - first].bitcast(FP8X4), h_sc[:, 2 * blk + half, i0:i0 + j1 - j0], h_cols(blk, j0, j1))
 
         y_ps = {}
 
@@ -259,9 +284,9 @@ def tile_list_regime_damped_signals_kernel(
         for kp in range(2):
             nc.vector.tensor_copy(v_codes[:, kp, :], v_win[kp][:].bitcast(U32).indirect(idx[:]))
 
-        round_wa(0, 0, "gpsimd")
+        round_wa(0, 0, "gpsimd", "wa_bf16_0")
         quantise_wa(0, 0, "v_win1")
-        round_wa(0, 1, "gpsimd")
+        round_wa(0, 1, "gpsimd", "wa_bf16_1")
         quantise_wa(0, 1, "g_win01")
         wf_codes = buffer("g_win01", [P, 2, N], I32, "wf_codes")
         nc.sync.dma_start(wf_codes[:], wf_words.rearrange("blk p n i -> p blk (n i)").bitcast(I32))
@@ -271,21 +296,17 @@ def tile_list_regime_damped_signals_kernel(
         loadings(0, "z")
         damped[0, 0] = buffer("g_win02", [P, 4, W], F32, "damped0")
         damp_loadings(0, [(0, W)])
-        gather_carry(0, 3, 0, W)
-        gather_carry(0, 3, W, S)
+        gather_carry(0, 3, 0, S)
         loadings(1, "x")
-        round_wa(1, 0, "gpsimd")
-        h_bf16[0, 0] = keep.tile([P, 4 * W], BF16, name="h_bf16_00", align_bytes=64)
+        round_wa(1, 0, "gpsimd", "wa_bf16_0")
+        quantise_wa(1, 0, "g_win03")
+        h_bf16[0, 0] = buffer("h_bf16_00", [P, 4 * Q], BF16, "h_bf16_0a")
         exposures(nc.gpsimd, 0, 0, Q)
-        for j0 in range(Q, W, E):
-            exposures(nc.gpsimd, 0, j0, j0 + E)
-        damped[1, 0] = buffer("g_win03", [P, 4, W], F32, "damped1")
+        damped[1, 0] = buffer("wa_bf16_0", [P, 4, W], F32, "damped1")
         damp_loadings(1, [(0, W)])
-        h_bf16[0, W] = buffer("h_bf16_01", [P, 4 * W], BF16, "h_bf16_01")
-        for j0 in range(W, S, E):
-            exposures(nc.gpsimd, 0, j0, j0 + E)
+        last = W + Q
 
-        round_wa(1, 1, "scalar")
+        round_wa(1, 1, "scalar", "wa_bf16_1")
         damp[2, 0] = buffer("wa_raw11", [P, 4, W], F32, "damp2")
         square(damp[2, 0][:], root2[:])
         root3 = buffer("root", [P, 4, W], F32, "root3")
@@ -295,21 +316,28 @@ def tile_list_regime_damped_signals_kernel(
         for i0 in (0, Q):
             damp[3, i0] = buffer("damp3_%d" % i0, [P, 4, Q], F32, "damp3_%d" % i0)
             square(damp[3, i0][:], root3[:, :, i0:i0 + Q])
-        quantise_wa(1, 0, "wa_codes10")
         quantise_wa(1, 1, "wa_codes11")
+        h_bf16[0, Q] = buffer("wa_bf16_1", [P, 4 * (Q + E)], BF16, "h_bf16_0b")
+        exposures(nc.gpsimd, 0, Q, W)
+        exposures(nc.gpsimd, 0, W, W + E)
         loadings(2, "x")
         damped[2, 0] = buffer("wa_raw00", [P, 4, LEAD], F32, "damped2_lead")
         damped[2, LEAD] = buffer("wa_raw01", [P, 4, W - LEAD], F32, "damped2_rest")
         damp_loadings(2, [(0, LEAD), (LEAD, W)])
-        loadings(3, "z")
+        loadings(3, "x")
+        h_bf16[0, last] = buffer("h_bf16_01", [P, 4 * Q], BF16, "h_bf16_0d")
+        exposures_on_tensor(0, last, "z")
         carry[1, 0] = buffer("carry1", [P, 4, W], F32, "carry1")
         for t in range(3):
             gather_carry(1, t, 0, W)
         for j0 in range(0, W, Q):
             gather_carry(1, 3, j0, j0 + Q)
         h_codes[0, 0] = buffer("wa_raw11", [P, W], U32, "h_codes00")[:]
-        quantise_h(0, 0, W)
-        open_signals(0, W, "x")
+        quantise_h(0, Q, W)
+        quantise_h(0, 0, Q)
+        h_bf16[0, W + E] = buffer("h_bf16_00", [P, 4 * E], BF16, "h_bf16_0c")
+        exposures(nc.gpsimd, 0, W + E, last)
+        open_signals(0, W, "z")
         h_bf16[1, 0] = buffer("h_bf16_10", [P, 4 * W], BF16, "h_bf16_10")
         for j0, j1 in ((0, LEAD), (LEAD, Q), (Q, W)):
             exposures(nc.gpsimd, 1, j0, j1)
@@ -322,19 +350,18 @@ def tile_list_regime_damped_signals_kernel(
         for t in range(4):
             gather_carry(1, t, W, W + Q)
         damp_loadings(3, [(Q, W)])
-        pair = buffer("wa_raw01", [P, 2, W], U32, "h_codes_pair")
-        h_codes[0, W] = pair[:, 0, :]
-        h_codes[1, 0] = pair[:, 1, :]
-        quantise_h(0, W, S)
+        h_codes[1, 0] = buffer("rounded%d" % E, [P, W], U32, "h_codes10")[:]
+        h_codes[0, W] = buffer("wa_raw01", [P, W], U32, "h_codes01")[:]
         quantise_h(1, 0, W)
+        for j0, j1 in ((W, W + E), (W + E, last), (last, S)):
+            quantise_h(0, j0, j1)
         signals(1, 0, W, 0, True)
         store(0, W, False)
-        h_bf16[1, W] = buffer("h_bf16_10", [P, 4 * Q], BF16, "h_bf16_third")
+        h_bf16[1, W] = buffer("h_bf16_01", [P, 4 * Q], BF16, "h_bf16_third")
         exposures(nc.gpsimd, 1, W, W + Q)
-        last = W + Q
-        carry[1, last] = buffer("h_bf16_01", [P, 4, Q], F32, "carry1_last")
-        open_signals(W, last, "z")
-        open_signals(last, S, "x")
+        carry[1, last] = buffer("h_bf16_10", [P, 4, Q], F32, "carry1_last")
+        open_signals(W, last, "x")
+        open_signals(last, S, "z")
         for t in range(4):
             gather_carry(1, t, last, S)
         h_codes[1, W] = buffer("g_win00", [P, Q], U32, "h_codes_third")[:]
@@ -342,7 +369,7 @@ def tile_list_regime_damped_signals_kernel(
         signals(1, W, last, W, True)
         store(W, last, False)
 
-        h_bf16[1, last] = buffer("h_bf16_10", [P, 4 * Q], BF16, "h_bf16_last")
+        h_bf16[1, last] = buffer("h_bf16_01", [P, 4 * Q], BF16, "h_bf16_last")
         for j0 in range(last, S, E):
             exposures(nc.vector, 1, j0, j0 + E)
         for j0, tag in ((last, "wa_raw10"), (last + E, "damp1")):

@@ -220,15 +220,14 @@ def tile_list_regime_damped_signals_kernel(
                     nc.tensor.matmul(sums[:, t, :], piece(carry, blk, j0 + e0, j0 + e0 + E)[:, t, :],
                                      ident[:], start=False, stop=True, is_transpose=True)
                 rounded.append(buffer("rounded%d" % e0, [P, W], BF16, "rounded%d" % e0))
-                nc.scalar.copy(rounded[-1][:].rearrange("j (w c i l) -> j w c l i", w=2, i=4, l=2),
-                               sums[:].rearrange("j (w l) (c i) -> j w c l i", w=2, i=4))
+                nc.scalar.copy(rounded[-1][:].rearrange("j (w p l) -> j w p l", w=2, l=2),
+                               sums[:].rearrange("j (w l) p -> j w p l", w=2))
             words = psum.tile([P, 2, 2, P], F32, name="words", tag=ring)
             for e in range(2):
                 for w in range(2):
                     nc.tensor.transpose(words[:, e, w, :], rounded[e][:].bitcast(F32)[:, P * w:P * (w + 1)], ident[:])
-            nc.scalar.copy(
-                h_cols(blk, j0, j0 + Q).bitcast(F32).rearrange("p (e c i w) -> p e c w i", e=2, i=4, w=2),
-                words[:].rearrange("p e w (c i) -> p e c w i", i=4))
+            nc.scalar.copy(h_cols(blk, j0, j0 + Q).bitcast(F32).rearrange("p (e j w) -> p e j w", e=2, w=2),
+                           words[:].rearrange("p e w j -> p e j w"))
 
         h_codes = {}
 
@@ -296,13 +295,14 @@ def tile_list_regime_damped_signals_kernel(
         loadings(0, "z")
         damped[0, 0] = buffer("g_win02", [P, 4, W], F32, "damped0")
         damp_loadings(0, [(0, W)])
-        gather_carry(0, 3, 0, S)
+        gather_carry(0, 3, 0, W)
+        gather_carry(0, 3, W, S)
         loadings(1, "x")
         round_wa(1, 0, "gpsimd", "wa_bf16_0")
-        quantise_wa(1, 0, "g_win03")
+        quantise_wa(1, 0, "wa_codes10")
         h_bf16[0, 0] = buffer("h_bf16_00", [P, 4 * Q], BF16, "h_bf16_0a")
         exposures(nc.gpsimd, 0, 0, Q)
-        damped[1, 0] = buffer("wa_bf16_0", [P, 4, W], F32, "damped1")
+        damped[1, 0] = buffer("g_win03", [P, 4, W], F32, "damped1")
         damp_loadings(1, [(0, W)])
         last = W + Q
 
@@ -369,7 +369,7 @@ def tile_list_regime_damped_signals_kernel(
         signals(1, W, last, W, True)
         store(W, last, False)
 
-        h_bf16[1, last] = buffer("h_bf16_01", [P, 4 * Q], BF16, "h_bf16_last")
+        h_bf16[1, last] = buffer("damp3_0", [P, 4 * Q], BF16, "h_bf16_last")
         for j0 in range(last, S, E):
             exposures(nc.vector, 1, j0, j0 + E)
         for j0, tag in ((last, "wa_raw10"), (last + E, "damp1")):

@@ -37,25 +37,25 @@ def tile_list_regime_damped_signals_kernel(
 
         idx = keep.tile([P, S // 16], U16, name="idx")
         idx2 = keep.tile([P, S // 16], U16, name="idx2")
-        v_sc_win = keep.tile([P, T // 4], I32, name="v_sc_win", align_bytes=64)
-        v2_sc_win = keep.tile([P, T // 4], I32, name="v2_sc_win", align_bytes=64)
-        wb_sc_raw = keep.tile([P, H // 4], I32, name="wb_sc_raw", align_bytes=64)
-        wf_sc = keep.tile([P, N // 4], I32, name="wf_sc", align_bytes=64)
-        wb_raw = keep.tile([P, H // 2], I32, name="wb_raw", align_bytes=64)
-        wb_codes = keep.tile([P, 2 * H], U8, name="wb_codes", align_bytes=64)
-        wb_sc = keep.tile([P, H], U8, name="wb_sc", align_bytes=64)
+        v_sc_win = keep.tile([P, T // 4], I32, name="v_sc_win", align_bytes=256)
+        v2_sc_win = keep.tile([P, T // 4], I32, name="v2_sc_win", align_bytes=256)
+        wb_sc_raw = keep.tile([P, H // 4], I32, name="wb_sc_raw", align_bytes=256)
+        wf_sc = keep.tile([P, N // 4], I32, name="wf_sc", align_bytes=256)
+        wb_raw = keep.tile([P, H // 2], I32, name="wb_raw", align_bytes=256)
+        wb_codes = keep.tile([P, 2 * H], U8, name="wb_codes", align_bytes=256)
+        wb_sc = keep.tile([P, H], U8, name="wb_sc", align_bytes=256)
         bias_t = keep.tile([P, 4], F32, name="bias_t")
         one = keep.tile([P, 1], F32, name="one")
         ident = keep.tile([P, P], F32, name="ident")
-        v_codes = keep.tile([P, 2, S], U32, name="v_codes", align_bytes=64)
-        v_sc = keep.tile([P, S], U8, name="v_sc", align_bytes=64)
-        v2_codes = keep.tile([P, S], U32, name="v2_codes", align_bytes=64)
-        v2_sc = keep.tile([P, S], U8, name="v2_sc", align_bytes=64)
-        wa_sc = keep.tile([P, 4, W], U8, name="wa_sc", align_bytes=64)
-        h_sc = keep.tile([P, 4, W], U8, name="h_sc", align_bytes=64)
+        v_codes = keep.tile([P, 2, S], U32, name="v_codes", align_bytes=256)
+        v_sc = keep.tile([P, S], U8, name="v_sc", align_bytes=256)
+        v2_codes = keep.tile([P, S], U32, name="v2_codes", align_bytes=256)
+        v2_sc = keep.tile([P, S], U8, name="v2_sc", align_bytes=256)
+        wa_sc = keep.tile([P, 4, W], U8, name="wa_sc", align_bytes=256)
+        h_sc = keep.tile([P, 4, W], U8, name="h_sc", align_bytes=256)
 
         def buffer(tag, shape, dtype, name):
-            return shared.tile(shape, dtype, name=name, tag=tag, align_bytes=64)
+            return shared.tile(shape, dtype, name=name, tag=tag, align_bytes=256)
 
         def half_cols(half):
             return slice(half * W, (half + 1) * W)
@@ -257,7 +257,7 @@ def tile_list_regime_damped_signals_kernel(
 
         def store(j0, j1, with_vector):
             for c in range(4):
-                y = work.tile([P, j1 - j0], F32, name="y", bufs=8)
+                y = work.tile([P, j1 - j0], F32, name="y", bufs=8, align_bytes=256)
                 if with_vector and c % 2 == 1:
                     nc.vector.tensor_scalar(y[:], y_ps[j0, c][:], bias_t[:, c:c + 1], None, ALU.add)
                 else:

@@ -67,6 +67,7 @@ def tile_list_regime_damped_signals_kernel(
             first = max(c for (k, c) in tiles if k == key and c <= c0)
             return tiles[key, first][:, :, c0 - first:c1 - first]
 
+        nc.vector.memset(v2_sc_win[:], 0)
         nc.vector.memset(v_sc_win[:], 0)
         nc.gpsimd.memset(wb_sc_raw[:], 0)
         nc.gpsimd.memset(one[:], 1.0)
@@ -96,10 +97,9 @@ def tile_list_regime_damped_signals_kernel(
                 nc.sync.dma_start(v_sc_win[p0:p0 + 4, :], tab_scales[kp, 4 * q:4 * q + 4, :].bitcast(I32))
 
         nc.sync.dma_start(idx2[:], offs2)
-        for q in range(4):
-            four = tab2_scales[0, 4 * q:4 * q + 4, :].bitcast(I32)
-            nc.sync.dma_start(v2_sc_win[32 * q:32 * q + 32, :], four.unsqueeze(0).broadcast_to([8, 4, T // 4]))
         nc.sync.dma_start(wb_raw[:], wb_words[0].bitcast(I32))
+        for q in range(4):
+            nc.sync.dma_start(v2_sc_win[32 * q:32 * q + 4, :], tab2_scales[0, 4 * q:4 * q + 4, :].bitcast(I32))
         v2_win = load_words("v2_win", tab2_words[0], "v2_win")
         nc.sync.dma_start(idx[:], offs)
         for q in range(4):

@@ -92,18 +92,17 @@ def tile_list_regime_damped_signals_kernel(
             nc.sync.dma_start(g_win[blk, t][:], gT_lanes[blk, t])
 
         def load_v_plane(kp):
-            for q in range(4):
-                p0 = 32 * q + 4 * (kp + 1)
-                nc.sync.dma_start(v_sc_win[p0:p0 + 4, :], tab_scales[kp, 4 * q:4 * q + 4, :].bitcast(I32))
+            for i in range(4):
+                nc.sync.dma_start(v_sc_win[4 * (kp + 1) + i:P:32, :], tab_scales[kp, i:16:4, :].bitcast(I32))
 
         nc.sync.dma_start(idx2[:], offs2)
         nc.sync.dma_start(wb_raw[:], wb_words[0].bitcast(I32))
-        for q in range(4):
-            nc.sync.dma_start(v2_sc_win[32 * q:32 * q + 4, :], tab2_scales[0, 4 * q:4 * q + 4, :].bitcast(I32))
+        for i in range(4):
+            nc.sync.dma_start(v2_sc_win[i:P:32, :], tab2_scales[0, i:16:4, :].bitcast(I32))
         v2_win = load_words("v2_win", tab2_words[0], "v2_win")
         nc.sync.dma_start(idx[:], offs)
-        for q in range(4):
-            nc.sync.dma_start(wb_sc_raw[32 * q:32 * q + 4, :], wb_scales[0, 4 * q:4 * q + 4, :].bitcast(I32))
+        for i in range(4):
+            nc.sync.dma_start(wb_sc_raw[i:P:32, :], wb_scales[0, i:16:4, :].bitcast(I32))
         v_win[0] = load_words("v_win0", tab_words[0], "v_win0")
         load_v_plane(0)
         load_wa("wa_raw00", 0, 0)

from contextlib import ExitStack

import concourse.mybir as mybir
from concourse.masks import make_identity

K, K2, H, N, T, S = 1024, 512, 1024, 512, 2048, 1024
FLOPS = 2 * S * (K * H + K2 * H + H * N)

F32 = mybir.dt.float32
BF16 = mybir.dt.bfloat16
I32 = mybir.dt.int32
U32 = mybir.dt.uint32
U16 = mybir.dt.uint16
U8 = mybir.dt.uint8
FP8X4 = mybir.dt.float8_e4m3fn_x4
FP4X4 = mybir.dt.float4_e2m1fn_x4
ACT = mybir.ActivationFunctionType
ALU = mybir.AluOpType

P = 128
W = 512
Q = 256
E = 128
LEAD = 32


def tile_list_regime_damped_signals_kernel(
    tc, wa, tab_words, tab_scales, tab2_words, tab2_scales, wb_words, wb_scales,
    wf_words, wf_scales, gT, bias, offs, offs2, out
):
    nc = tc.nc
    with ExitStack() as ctx:
        keep = ctx.enter_context(tc.tile_pool(name="keep", bufs=1))
        shared = ctx.enter_context(tc.tile_pool(name="shared", bufs=1))
        work = ctx.enter_context(tc.tile_pool(name="work", bufs=2))
        psum = ctx.enter_context(tc.psum_pool(name="psum", bufs=4))

        idx = keep.tile([P, S // 16], U16, name="idx")
        idx2 = keep.tile([P, S // 16], U16, name="idx2")
        v_sc_win = keep.tile([P, T // 4], I32, name="v_sc_win", align_bytes=256)
        v2_sc_win = keep.tile([P, T // 4], I32, name="v2_sc_win", align_bytes=256)
        wb_sc_raw = keep.tile([P, H // 4], I32, name="wb_sc_raw", align_bytes=256)
        wf_sc = keep.tile([P, N // 4], I32, name="wf_sc", align_bytes=256)
        wb_raw = keep.tile([P, H // 2], I32, name="wb_raw", align_bytes=256)
        wb_codes = keep.tile([P, 2 * H], U8, name="wb_codes", align_bytes=256)
        wb_sc = keep.tile([P, H], U8, name="wb_sc", align_bytes=256)
        bias_t = keep.tile([P, 4], F32, name="bias_t")
        one = keep.tile([P, 1], F32, name="one")
        ident = keep.tile([P, P], F32, name="ident")
        v_codes = keep.tile([P, 2, S], U32, name="v_codes", align_bytes=256)
        v_sc = keep.tile([P, S], U8, name="v_sc", align_bytes=256)
        v2_codes = keep.tile([P, S], U32, name="v2_codes", align_bytes=256)
        v2_sc = keep.tile([P, S], U8, name="v2_sc", align_bytes=256)
        wa_sc = keep.tile([P, 4, W], U8, name="wa_sc", align_bytes=256)
        h_sc = keep.tile([P, 4, W], U8, name="h_sc", align_bytes=256)

        def buffer(tag, shape, dtype, name):
            return shared.tile(shape, dtype, name=name, tag=tag, align_bytes=256)

        def half_cols(half):
            return slice(half * W, (half + 1) * W)

        def entries(lst, j0, j1):
            return lst[:, j0 // 16:j1 // 16]

        def piece(tiles, key, c0, c1):
            first = max(c for (k, c) in tiles if k == key and c <= c0)
            return tiles[key, first][:, :, c0 - first:c1 - first]

        nc.vector.memset(v2_sc_win[:], 0)
        nc.vector.memset(v_sc_win[:], 0)
        nc.gpsimd.memset(wb_sc_raw[:], 0)
        nc.gpsimd.memset(one[:], 1.0)
        nc.gpsimd.memset(wf_sc[:], 0)
        make_identity(nc, ident[:])

        wa_raw, g_win, v_win = {}, {}, {}
        gT_lanes = gT.rearrange("(blk p t) j -> blk t p j", blk=2, t=4)
        wa_rows = wa.rearrange("(kp p i) r -> kp p i r", kp=2, i=4)

        def load_words(tag, words, name):
            win = buffer(tag, [P, T], I32, name)
            nc.sync.dma_start(win[:], words.rearrange("p j i -> p (j i)").bitcast(I32))
            return win

        def load_wa(tag, blk, kp):
            wa_raw[blk, kp] = buffer(tag, [P, 4, W], F32, "wa_raw%d%d" % (blk, kp))
            nc.sync.dma_start(wa_raw[blk, kp][:], wa_rows[kp, :, :, blk * W:(blk + 1) * W])

        def load_g(tag, blk, t):
            g_win[blk, t] = buffer(tag, [P, T], F32, "g_win%d%d" % (blk, t))
            nc.sync.dma_start(g_win[blk, t][:], gT_lanes[blk, t])

        def load_v_plane(kp):
            for i in range(4):
                nc.sync.dma_start(v_sc_win[4 * (kp + 1) + i:P:32, :], tab_scales[kp, i:16:4, :].bitcast(I32))

        nc.sync.dma_start(idx2[:], offs2)
        nc.sync.dma_start(wb_raw[:], wb_words[0].bitcast(I32))
        for i in range(4):
            nc.sync.dma_start(v2_sc_win[i:P:32, :], tab2_scales[0, i:16:4, :].bitcast(I32))
        v2_win = load_words("v2_win", tab2_words[0], "v2_win")
        nc.sync.dma_start(idx[:], offs)
        for i in range(4):
            nc.sync.dma_start(wb_sc_raw[i:P:32, :], wb_scales[0, i:16:4, :].bitcast(I32))
        v_win[0] = load_words("v_win0", tab_words[0], "v_win0")
        load_v_plane(0)
        load_wa("wa_raw00", 0, 0)
        load_v_plane(1)
        v_win[1] = load_words("v_win1", tab_words[1], "v_win1")
        load_g("g_win00", 0, 0)
        load_wa("wa_raw01", 0, 1)
        load_g("g_win01", 0, 1)
        load_g("g_win02", 0, 2)
        load_wa("wa_raw10", 1, 0)
        load_g("g_win03", 0, 3)
        load_wa("wa_raw11", 1, 1)
        load_g("v2_win", 1, 0)
        load_g("v_win0", 1, 1)
        load_g("g_win12", 1, 2)
        load_g("g_win00", 1, 3)
        for q in range(4):
            nc.sync.dma_start(wf_sc[32 * q:32 * q + 8, :], wf_scales[:, 4 * q:4 * q + 4, :].bitcast(I32))
        with nc.allow_non_contiguous_dma(reason="one bias value a partition"):
            nc.sync.dma_start(bias_t[:], bias.rearrange("(c p) -> p c", p=P))

        def reorder_wb(blk):
            nc.vector.tensor_copy(
                wb_codes[:].bitcast(U16)[:, half_cols(blk)].rearrange("p (t m) -> p t m", t=4),
                wb_raw[:].bitcast(U16)[:, half_cols(blk)].rearrange("p (m t) -> p t m", t=4))
            nc.gpsimd.tensor_copy(
                wb_sc[:, half_cols(blk)].rearrange("p (t m) -> p t m", t=4),
                wb_sc_raw[:].bitcast(U8)[:, half_cols(blk)].rearrange("p (m t) -> p t m", t=4))

        damp = {}

        def stress(u, ring, dst):
            blk, half = divmod(u, 2)
            for t in range(4):
                c = 4 * blk + t
                b_ps = psum.tile([P, W], F32, name="b_ps", tag=ring)
                nc.tensor.matmul_mx(
                    b_ps[:], lhsT=wb_codes[:, 2 * P * c:2 * P * (c + 1)].bitcast(FP4X4),
                    lhsT_scale=wb_sc[:, P * c:P * (c + 1)],
                    rhs=v2_codes[:, half_cols(half)].bitcast(FP8X4), rhs_scale=v2_sc[:, half_cols(half)],
                    start=True, stop=True)
                nc.scalar.activation(dst[:, t, :], b_ps[:], ACT.Abs)

        def take_root(run):
            nc.scalar.activation(run, run, ACT.Abs_reciprocal_sqrt, bias=one[:])

        def square(dst, src):
            nc.scalar.activation(dst, src, ACT.Square)

        wa_bf16, wa_codes = {}, {}

        def round_wa(blk, kp, eng, tag):
            wa_bf16[blk, kp] = buffer(tag, [P, 4 * W], BF16, "wa_bf16_%d%d" % (blk, kp))
            dst = wa_bf16[blk, kp][:].rearrange("p (t m i) -> p m t i", t=4, i=4)
            src = wa_raw[blk, kp][:].rearrange("p i (m t) -> p m t i", t=4)
            if eng == "gpsimd":
                nc.gpsimd.tensor_scalar(dst, src, 1.0, 0.0, ALU.mult, ALU.add)
            else:
                nc.scalar.copy(dst, src)

        def quantise_wa(blk, kp, tag):
            wa_codes[blk, kp] = buffer(tag, [P, W], U32, "wa_codes%d%d" % (blk, kp))
            nc.vector.quantize_mx(wa_codes[blk, kp][:].bitcast(FP8X4), wa_sc[:, 2 * blk + kp, :], wa_bf16[blk, kp][:])

        carry = {}

        def gather_carry(blk, t, j0, j1):
            nc.vector.tensor_copy(piece(carry, blk, j0, j1)[:, t, :], g_win[blk, t][:].indirect(entries(idx, j0, j1)))

        a_ps = {}

        def loadings(u, ring):
            blk, half = divmod(u, 2)
            passes = (1, 0) if half else (0, 1)
            for t in range(4):
                a_ps[u, t] = psum.tile([P, W], F32, name="a_ps", tag=ring)
                for kp in passes:
                    nc.tensor.matmul_mx(
                        a_ps[u, t][:], lhsT=wa_codes[blk, kp][:, P * t:P * (t + 1)].bitcast(FP8X4),
                        lhsT_scale=wa_sc[:, 2 * blk + kp, P * t:P * (t + 1)],
                        rhs=v_codes[:, kp, half_cols(half)].bitcast(FP8X4),
                        rhs_scale=v_sc[4 * (kp + 1):P, half_cols(half)],
                        start=(kp == passes[0]), stop=(kp == passes[1]))

        damped = {}

        def damp_loadings(u, ranges):
            for t in range(4):
                for i0, i1 in ranges:
                    nc.vector.tensor_tensor(
                        damped[u, i0][:, t, :], a_ps[u, t][:, i0:i1], piece(damp, u, i0, i1)[:, t, :], ALU.mult)

        h_bf16 = {}

        def h_cols(blk, j0, j1):
            first = max(j for (b, j) in h_bf16 if b == blk and j <= j0)
            return h_bf16[blk, first][:, 4 * (j0 - first):4 * (j1 - first)]

        def exposures(eng, blk, j0, j1):
            half, i0 = divmod(j0, W)
            eng.tensor_tensor(
                h_cols(blk, j0, j1).rearrange("p (c i t) -> p c t i", i=4, t=4),
                piece(damped, 2 * blk + half, i0, i0 + j1 - j0).rearrange("p t (c i) -> p c t i", i=4),
                piece(carry, blk, j0, j1).rearrange("p t (c i) -> p c t i", i=4), ALU.add)

        def exposures_on_tensor(blk, j0, ring):
            half, i0 = divmod(j0, W)
            rounded = []
            for e0 in (0, E):
                sums = psum.tile([P, 4, P], F32, name="sums", tag=ring)
                for t in range(4):
                    nc.tensor.matmul(sums[:, t, :], piece(damped, 2 * blk + half, i0 + e0, i0 + e0 + E)[:, t, :],
                                     ident[:], start=True, stop=False, is_transpose=True)
                    nc.tensor.matmul(sums[:, t, :], piece(carry, blk, j0 + e0, j0 + e0 + E)[:, t, :],
                                     ident[:], start=False, stop=True, is_transpose=True)
                rounded.append(buffer("rounded%d" % e0, [P, W], BF16, "rounded%d" % e0))
                nc.scalar.copy(rounded[-1][:].rearrange("j (w p l) -> j w p l", w=2, l=2),
                               sums[:].rearrange("j (w l) p -> j w p l", w=2))
            words = psum.tile([P, 2, 2, P], F32, name="words", tag=ring)
            for e in range(2):
                for w in range(2):
                    nc.tensor.transpose(words[:, e, w, :], rounded[e][:].bitcast(F32)[:, P * w:P * (w + 1)], ident[:])
            nc.scalar.copy(h_cols(blk, j0, j0 + Q).bitcast(F32).rearrange("p (e j w) -> p e j w", e=2, w=2),
                           words[:].rearrange("p e w j -> p e j w"))

        h_codes = {}

        def quantise_h(blk, j0, j1):
            half, i0 = divmod(j0, W)
            first = max(j for (b, j) in h_codes if b == blk and j <= j0)
            nc.vector.quantize_mx(
                h_codes[blk, first][:, j0 - first:j1 - first].bitcast(FP8X4), h_sc[:, 2 * blk + half, i0:i0 + j1 - j0], h_cols(blk, j0, j1))

        y_ps = {}

        def signals(blk, j0, j1, y0, stop):
            half, i0 = divmod(j0, W)
            first = max(j for (b, j) in h_codes if b == blk and j <= j0)
            for c in range(4):
                nc.tensor.matmul_mx(
                    y_ps[y0, c][:, j0 - y0:j1 - y0], lhsT=wf_codes[:, blk, P * c:P * (c + 1)].bitcast(FP8X4),
                    lhsT_scale=wf_sc[:].bitcast(U8)[4 * blk:P, P * c:P * (c + 1)],
                    rhs=h_codes[blk, first][:, j0 - first:j1 - first].bitcast(FP8X4),
                    rhs_scale=h_sc[:, 2 * blk + half, i0:i0 + j1 - j0],
                    start=(blk == 0), stop=stop)

        def open_signals(j0, j1, ring):
            for c in range(4):
                y_ps[j0, c] = psum.tile([P, j1 - j0], F32, name="y_ps", tag=ring)
            signals(0, j0, j1, j0, False)

        def store(j0, j1, with_vector):
            for c in range(4):
                y = work.tile([P, j1 - j0], F32, name="y", bufs=8, align_bytes=256)
                if with_vector and c % 2 == 1:
                    nc.vector.tensor_scalar(y[:], y_ps[j0, c][:], bias_t[:, c:c + 1], None, ALU.add)
                else:
                    nc.scalar.activation(y[:], y_ps[j0, c][:], ACT.Identity, bias=bias_t[:, c:c + 1])
                nc.sync.dma_start(out[P * c:P * (c + 1), j0:j1], y[:])

        nc.vector.tensor_copy(v2_sc[:], v2_sc_win[:].bitcast(U8).indirect(idx2[:]))
        for half in range(2):
            reorder_wb(half)
            nc.vector.tensor_copy(
                v2_codes[:, half_cols(half)], v2_win[:].bitcast(U32).indirect(entries(idx2, half * W, (half + 1) * W)))
        for u, ring in ((0, "x"), (1, "z")):
            damp[u, 0] = buffer("damp%d" % u, [P, 4, W], F32, "damp%d" % u)
            stress(u, ring, damp[u, 0])
        for u in range(2):
            take_root(damp[u, 0][:])
        for u in range(2):
            square(damp[u, 0][:], damp[u, 0][:])
        root2 = buffer("root", [P, 4, W], F32, "root2")
        stress(2, "x", root2)
        take_root(root2[:])
        nc.vector.tensor_copy(v_sc[:], v_sc_win[:].bitcast(U8).indirect(idx[:]))
        for kp in range(2):
            nc.vector.tensor_copy(v_codes[:, kp, :], v_win[kp][:].bitcast(U32).indirect(idx[:]))

        round_wa(0, 0, "gpsimd", "wa_bf16_0")
        quantise_wa(0, 0, "v_win1")
        round_wa(0, 1, "gpsimd", "wa_bf16_1")
        quantise_wa(0, 1, "g_win01")
        wf_codes = buffer("g_win01", [P, 2, N], I32, "wf_codes")
        nc.sync.dma_start(wf_codes[:], wf_words.rearrange("blk p n i -> p blk (n i)").bitcast(I32))
        carry[0, 0] = keep.tile([P, 4, S], F32, name="carry0")
        for t in range(3):
            gather_carry(0, t, 0, S)
        loadings(0, "z")
        damped[0, 0] = buffer("g_win02", [P, 4, W], F32, "damped0")
        damp_loadings(0, [(0, W)])
        gather_carry(0, 3, 0, W)
        gather_carry(0, 3, W, S)
        loadings(1, "x")
        round_wa(1, 0, "gpsimd", "wa_bf16_0")
        quantise_wa(1, 0, "wa_codes10")
        h_bf16[0, 0] = buffer("h_bf16_00", [P, 4 * Q], BF16, "h_bf16_0a")
        exposures(nc.gpsimd, 0, 0, Q)
        damped[1, 0] = buffer("g_win03", [P, 4, W], F32, "damped1")
        damp_loadings(1, [(0, W)])
        last = W + Q

        round_wa(1, 1, "scalar", "wa_bf16_1")
        damp[2, 0] = buffer("wa_raw11", [P, 4, W], F32, "damp2")
        square(damp[2, 0][:], root2[:])
        root3 = buffer("root", [P, 4, W], F32, "root3")
        stress(3, "z", root3)
        for i0 in (0, Q):
            take_root(root3[:, :, i0:i0 + Q])
        for i0 in (0, Q):
            damp[3, i0] = buffer("damp3_%d" % i0, [P, 4, Q], F32, "damp3_%d" % i0)
            square(damp[3, i0][:], root3[:, :, i0:i0 + Q])
        quantise_wa(1, 1, "wa_codes11")
        h_bf16[0, Q] = buffer("wa_bf16_1", [P, 4 * (Q + E)], BF16, "h_bf16_0b")
        exposures(nc.gpsimd, 0, Q, W)
        exposures(nc.gpsimd, 0, W, W + E)
        loadings(2, "x")
        damped[2, 0] = buffer("wa_raw00", [P, 4, LEAD], F32, "damped2_lead")
        damped[2, LEAD] = buffer("wa_raw01", [P, 4, W - LEAD], F32, "damped2_rest")
        damp_loadings(2, [(0, LEAD), (LEAD, W)])
        loadings(3, "x")
        h_bf16[0, last] = buffer("h_bf16_01", [P, 4 * Q], BF16, "h_bf16_0d")
        exposures_on_tensor(0, last, "z")
        carry[1, 0] = buffer("carry1", [P, 4, W], F32, "carry1")
        for t in range(3):
            gather_carry(1, t, 0, W)
        for j0 in range(0, W, Q):
            gather_carry(1, 3, j0, j0 + Q)
        h_codes[0, 0] = buffer("wa_raw11", [P, W], U32, "h_codes00")[:]
        quantise_h(0, Q, W)
        quantise_h(0, 0, Q)
        h_bf16[0, W + E] = buffer("h_bf16_00", [P, 4 * E], BF16, "h_bf16_0c")
        exposures(nc.gpsimd, 0, W + E, last)
        open_signals(0, W, "z")
        h_bf16[1, 0] = buffer("h_bf16_10", [P, 4 * W], BF16, "h_bf16_10")
        for j0, j1 in ((0, LEAD), (LEAD, Q), (Q, W)):
            exposures(nc.gpsimd, 1, j0, j1)

        damped3 = buffer("wa_raw00", [P, 2, 4, Q], F32, "damped3")
        damped[3, 0] = damped3[:, 0]
        damped[3, Q] = damped3[:, 1]
        damp_loadings(3, [(0, Q)])
        carry[1, W] = buffer("damp3_0", [P, 4, Q], F32, "carry1_third")
        for t in range(4):
            gather_carry(1, t, W, W + Q)
        damp_loadings(3, [(Q, W)])
        h_codes[1, 0] = buffer("rounded%d" % E, [P, W], U32, "h_codes10")[:]
        h_codes[0, W] = buffer("wa_raw01", [P, W], U32, "h_codes01")[:]
        quantise_h(1, 0, W)
        for j0, j1 in ((W, W + E), (W + E, last), (last, S)):
            quantise_h(0, j0, j1)
        signals(1, 0, W, 0, True)
        store(0, W, False)
        h_bf16[1, W] = buffer("h_bf16_01", [P, 4 * Q], BF16, "h_bf16_third")
        exposures(nc.gpsimd, 1, W, W + Q)
        carry[1, last] = buffer("h_bf16_10", [P, 4, Q], F32, "carry1_last")
        open_signals(W, last, "x")
        open_signals(last, S, "z")
        for t in range(4):
            gather_carry(1, t, last, S)
        h_codes[1, W] = buffer("g_win00", [P, Q], U32, "h_codes_third")[:]
        quantise_h(1, W, last)
        signals(1, W, last, W, True)
        store(W, last, False)

        h_bf16[1, last] = buffer("damp3_0", [P, 4 * Q], BF16, "h_bf16_last")
        for j0 in range(last, S, E):
            exposures(nc.vector, 1, j0, j0 + E)
        for j0, tag in ((last, "wa_raw10"), (last + E, "damp1")):
            h_codes[1, j0] = buffer(tag, [P, E], U32, "h_codes1_%d" % j0)[:]
            quantise_h(1, j0, j0 + E)
        for j0 in range(last, S, E):
            signals(1, j0, j0 + E, last, j0 + E == S)
        store(last, S, True)
